import numpy as np
import ml_dtypes


def mxq(x, axis, fmt="e4m3"):
    dtype, down = {"e4m3": (ml_dtypes.float8_e4m3fn, 7), "e5m2": (ml_dtypes.float8_e5m2, 14)}[fmt]
    v = np.moveaxis(np.asarray(x, np.float32).astype(ml_dtypes.bfloat16).astype(np.float64), axis, -1)
    blocks = v.reshape(v.shape[:-1] + (-1, 32))
    amax = np.abs(blocks).max(-1, keepdims=True)
    byte = np.maximum(np.where(amax > 0, np.frexp(amax)[1] - 1 + 127, 0) - down, 1)
    scale = np.exp2(byte - 127.0)
    codes = (blocks / scale).astype(np.float32).astype(dtype).astype(np.float64)
    return np.moveaxis((codes * scale).reshape(v.shape), -1, axis)


WIDE = False


def mx_kscale(k):
    if not WIDE:
        return np.ones(k)
    levels = np.array([10, -10, 5, -5, 0])
    if k % 512:
        return np.exp2(np.random.permutation(np.resize(levels, k // 32))).repeat(32)
    a = np.empty((k // 512, 16))
    for p in range(k // 512):
        a[p, :8] = np.random.permutation(np.resize(levels, 8))
        for g in range(8):
            far = levels[np.abs(levels - a[p, g]) >= 10]
            a[p, g + 8] = far[np.random.randint(len(far))]
    return np.exp2(a.ravel()).repeat(32)


def f64(x):
    return np.asarray(x).astype(np.float64)


def striped(idx):
    return np.tile(idx.reshape(-1, 16).T, (8, 1)).astype(np.uint16)


def unstriped(offs):
    return offs[:16].T.reshape(-1).astype(np.int64)


E2M1 = np.array([0.0, 0.5, 1.0, 1.5, 2.0, 3.0, 4.0, 6.0, -0.0, -0.5, -1.0, -1.5, -2.0, -3.0, -4.0, -6.0])


def pack_weight(w, fmt):
    k, n = w.shape
    w = f64(np.asarray(w, np.float32).astype(ml_dtypes.bfloat16)).reshape(k // 32, 32, n)
    amax = np.abs(w).max(1)
    if fmt == "e4m3":
        byte = np.frexp(amax)[1] - 1 + 127 - 7
    else:
        mant, ex = np.frexp(amax / 6.0)
        byte = np.where(mant > 0.5, ex, ex - 1) + 127
    byte = np.clip(np.where(amax > 0, byte, 1), 1, 254)
    scaled = (w * np.exp2(127.0 - byte)[:, None, :]).reshape(k, n).astype(np.float32)
    by_word = np.ascontiguousarray(scaled.reshape(k // 512, 128, 4, n).transpose(0, 1, 3, 2))
    if fmt == "e4m3":
        words = by_word.astype(ml_dtypes.float8_e4m3fn).view(np.uint8)
    else:
        c = by_word.astype(ml_dtypes.float4_e2m1fn).view(np.uint8) & 0xF
        words = (c[..., 0::2] | (c[..., 1::2] << 4)).reshape(k // 512, 128, 2 * n)
    return np.ascontiguousarray(words), np.ascontiguousarray(byte.astype(np.uint8).reshape(k // 512, 16, n))


def unpack_weight(words, scales, fmt):
    g, _, n = scales.shape
    words = np.ascontiguousarray(words).reshape(g, 128, n, -1)
    if fmt == "e4m3":
        vals = words.view(ml_dtypes.float8_e4m3fn).astype(np.float64)
    else:
        nib = np.empty((g, 128, n, 4), np.uint8)
        nib[..., 0::2] = words & 0xF
        nib[..., 1::2] = words >> 4
        vals = E2M1[nib]
    vals = vals * np.repeat(np.exp2(scales.astype(np.float64) - 127.0), 8, axis=1)[..., None]
    return vals.transpose(0, 1, 3, 2).reshape(g * 512, n)


def relu2(v):
    return np.maximum(v, 0.0) ** 2


K, T, E, C, N = 2560, 768, 6, 128, 128
TOP = 3
PAD = 64


def by_expert(wq, xq):
    return np.concatenate([wq[e].T @ xq[:, e * C:(e + 1) * C] for e in range(E)], axis=1)


def setup_inputs():
    n = np.random.standard_normal
    s = mx_kscale(K)[:, None]
    slot_token = np.empty(E * C, np.int64); pos = np.tile(E * C + np.arange(T) % PAD, (TOP, 1)); taken = np.zeros(T, np.int64)
    liked = np.random.randn(T)
    for e in np.random.permutation(E):
        free = np.flatnonzero(taken < TOP); pick = np.random.permutation(free[np.argsort(-(liked[free] + np.random.gumbel(size=free.size)))[:C]]); slot_token[e * C:(e + 1) * C] = pick
        pos[taken[pick], pick] = e * C + np.arange(C); taken[pick] += 1
    g = np.random.uniform(0.2, 0.8, (TOP, T))
    w = [pack_weight(m, "e2m1") for m in n((E, K, N)) / np.sqrt(K) / s[None]]
    return {
        "xT": (n((K, T)) * s).astype(np.float32),
        "w_words": np.stack([m[0] for m in w]),
        "w_scales": np.stack([m[1] for m in w]),
        "b": (0.3 * n((N, E))).astype(np.float32),
        "gate": np.stack([np.tile(r, (N, 1)) for r in g]).astype(np.float32),
        "offs": striped(slot_token),
        "pos1": striped(pos[0]),
        "pos2": striped(pos[1]),
        "pos3": striped(pos[2]),
    }


def reference(xT, w_words, w_scales, b, gate, offs, pos1, pos2, pos3):
    idx = unstriped(offs)
    w = np.stack([unpack_weight(w_words[e], w_scales[e], "e2m1") for e in range(E)])
    xq = mxq(f64(xT)[:, idx], 0, "e4m3")
    y = by_expert(w, xq)
    y = relu2(y + np.repeat(f64(b), C, axis=1))
    y = np.concatenate([y, np.zeros((N, PAD))], axis=1)
    return sum(f64(gate[r]) * y[:, unstriped(p)] for r, p in enumerate((pos1, pos2, pos3)))

@@ -1,0 +1,130 @@
+from contextlib import ExitStack
+
+import concourse.mybir as mybir
+
+K, T, E, C, N = 2560, 768, 6, 128, 128
+SLOTS = E * C
+PAD = 64
+FLOPS = 2 * K * N * SLOTS
+
+F32 = mybir.dt.float32
+BF16 = mybir.dt.bfloat16
+I32 = mybir.dt.int32
+U32 = mybir.dt.uint32
+U16 = mybir.dt.uint16
+U8 = mybir.dt.uint8
+FP8X4 = mybir.dt.float8_e4m3fn_x4
+FP4X4 = mybir.dt.float4_e2m1fn_x4
+ACT = mybir.ActivationFunctionType
+ALU = mybir.AluOpType
+
+P = 128
+PACK = 4
+K_PASS = P * PACK
+PASSES = K // K_PASS
+LIST_COL = 16
+
+
+def pieces(widths):
+    out, start = [], 0
+    for w in widths:
+        out.append((start, start + w))
+        start = start + w
+    return out
+
+
+def tile_moe_ecr_lin_relu2_kernel(tc, xT, w_words, w_scales, b, gate, offs, pos1, pos2, pos3, out):
+    nc = tc.nc
+    token_cuts = [pieces([256, 256, 256]), pieces([256, 256, 256]), pieces([512, 256]), pieces([512, 256]), pieces([512, 256])]
+    slot_cuts = [pieces([384, 384])] * (PASSES - 1) + [pieces([384, 256, 128])]
+    out_cuts = pieces([512, 256])
+
+    with ExitStack() as ctx:
+        lists = ctx.enter_context(tc.tile_pool(name="lists", bufs=1))
+        keep = ctx.enter_context(tc.tile_pool(name="keep", bufs=1))
+        psum = ctx.enter_context(tc.psum_pool(name="psum", bufs=1))
+
+        slot_tokens = lists.tile([P, SLOTS // LIST_COL], U16, name="slot_tokens")
+        token_slots = [lists.tile([P, T // LIST_COL], U16, name=f"token_slots{r}") for r in range(3)]
+
+        token_scales = [keep.tile([P, T], U8, name=f"token_scales{a}", align_bytes=64) for a in range(PASSES)]
+        token_codes = [keep.tile([P, T], U32, name=f"token_codes{a}", align_bytes=64) for a in range(PASSES)]
+        weight_scales = keep.tile([P, E * PASSES * N], U8, name="weight_scales", align_bytes=64)
+        y = keep.tile([P, SLOTS + PAD], F32, name="y")
+        for a in range(PASSES):
+            nc.vector.memset(token_scales[a][:].bitcast(I32), 0)
+        nc.vector.memset(weight_scales[:].bitcast(I32), 0)
+        nc.vector.memset(y[:, SLOTS:], 0.0)
+
+        raw = {}
+        for a in range(PASSES):
+            rows = xT[a * K_PASS:(a + 1) * K_PASS, :].rearrange("(p j) t -> p j t", j=PACK)
+            for t0, t1 in token_cuts[a]:
+                raw[a, t0] = keep.tile([P, PACK, t1 - t0], F32, name=f"raw{a}_{t0}")
+                nc.sync.dma_start(out=raw[a, t0][:], in_=rows[:, :, t0:t1])
+            if a == 0:
+                nc.sync.dma_start(slot_tokens[:], offs)
+        scale_rows = w_scales.bitcast(I32).rearrange("e a (q r) n -> r q (e a) n", r=4)
+        for r in range(4):
+            nc.sync.dma_start(
+                out=weight_scales[r:P:32, :].bitcast(I32).rearrange("q (g n) -> q g n", g=E * PASSES), in_=scale_rows[r])
+        weight_codes = []
+        for a in range(PASSES):
+            wt = keep.tile([P, E * 2 * N], U8, name=f"weight_codes{a}", align_bytes=64)
+            nc.sync.dma_start(out=wt[:].bitcast(I32).rearrange("p (e c) -> p e c", e=E),
+                              in_=w_words.bitcast(I32)[:, a].rearrange("e p c -> p e c"))
+            weight_codes.append(wt)
+        bias = keep.tile([P, E], F32, name="bias")
+        nc.sync.dma_start(out=bias[:], in_=b)
+        for tile, src in zip(token_slots, (pos1, pos2, pos3)):
+            nc.sync.dma_start(tile[:], src)
+        gates = [keep.tile([P, T], F32, name=f"gate{r}") for r in range(3)]
+        for r in range(3):
+            nc.sync.dma_start(out=gates[r][:], in_=gate[r])
+
+        sums = [psum.tile([P, C], F32, name=f"sums{e}") for e in range(E)]
+
+        for a in range(PASSES):
+            for t0, t1 in token_cuts[a]:
+                grouped = keep.tile([P, t1 - t0, PACK], BF16, name=f"grouped{a}_{t0}", align_bytes=64)
+                dst = grouped[:].rearrange("p (c i) j -> p c j i", i=4)
+                src = raw[a, t0][:].rearrange("p j (c i) -> p c j i", i=4)
+                if a == 0 and t1 == T:
+                    nc.vector.tensor_copy(out=dst, in_=src)
+                else:
+                    nc.scalar.activation(out=dst, in_=src, func=ACT.Copy)
+                nc.vector.quantize_mx(out=token_codes[a][:, t0:t1].bitcast(FP8X4), scales=token_scales[a][:, t0:t1],
+                                      in_=grouped[:].rearrange("p t j -> p (t j)"))
+            for s0, s1 in slot_cuts[a]:
+                picks = slot_tokens[:, s0 // LIST_COL:s1 // LIST_COL]
+                codes = keep.tile([P, s1 - s0], U32, name=f"slot_codes{a}_{s0}", align_bytes=64)
+                scales = keep.tile([P, s1 - s0], U8, name=f"slot_scales{a}_{s0}", align_bytes=64)
+                nc.vector.tensor_copy(codes[:], token_codes[a][:].indirect(picks))
+                nc.vector.tensor_copy(scales[:], token_scales[a][:].indirect(picks))
+                for e in range(s0 // C, s1 // C):
+                    cols = slice(e * C - s0, (e + 1) * C - s0)
+                    g = e * PASSES + a
+                    nc.tensor.matmul_mx(
+                        out=sums[e][:],
+                        lhsT=weight_codes[a][:, e * 2 * N:(e + 1) * 2 * N].bitcast(FP4X4),
+                        lhsT_scale=weight_scales[:, g * N:(g + 1) * N],
+                        rhs=codes[:, cols].bitcast(FP8X4),
+                        rhs_scale=scales[:, cols],
+                        start=(a == 0), stop=(a == PASSES - 1))
+
+        for s0, s1 in slot_cuts[-1]:
+            clipped = keep.tile([P, s1 - s0], F32, name=f"clipped{s0}")
+            for e in range(s0 // C, s1 // C):
+                nc.scalar.activation(out=clipped[:, e * C - s0:(e + 1) * C - s0], in_=sums[e][:], func=ACT.Relu, bias=bias[:, e:e + 1])
+            nc.scalar.activation(out=y[:, s0:s1], in_=clipped[:], func=ACT.Square)
+
+        for t0, t1 in out_cuts:
+            terms = [keep.tile([P, t1 - t0], F32, name=f"term{r}_{t0}") for r in range(3)]
+            for r in range(3):
+                nc.vector.tensor_tensor(terms[r][:], y[:].indirect(token_slots[r][:, t0 // LIST_COL:t1 // LIST_COL]),
+                                        gates[r][:, t0:t1], ALU.mult)
+            two = keep.tile([P, t1 - t0], F32, name=f"two{t0}")
+            total = keep.tile([P, t1 - t0], F32, name=f"total{t0}")
+            nc.vector.tensor_tensor(two[:], terms[0][:], terms[1][:], ALU.add)
+            nc.vector.tensor_tensor(total[:], two[:], terms[2][:], ALU.add)
+            nc.sync.dma_start(out=out[:, t0:t1], in_=total[:])

@@ -1,6 +1,7 @@
 from contextlib import ExitStack
 
 import concourse.mybir as mybir
+from concourse.masks import make_identity
 
 K, T, E, C, N = 2560, 768, 6, 128, 128
 SLOTS = E * C
@@ -22,7 +23,11 @@ P = 128
 PACK = 4
 K_PASS = P * PACK
 PASSES = K // K_PASS
+LAST = PASSES - 1
 LIST_COL = 16
+WINDOW = 1024
+MOVED_ROWS = 112
+CHUNK = 256
 
 
 def pieces(widths):
@@ -35,9 +40,9 @@ def pieces(widths):
 
 def tile_moe_ecr_lin_relu2_kernel(tc, xT, w_words, w_scales, b, gate, offs, pos1, pos2, pos3, out):
     nc = tc.nc
-    token_cuts = [pieces([256, 256, 256]), pieces([256, 256, 256]), pieces([512, 256]), pieces([512, 256]), pieces([512, 256])]
-    slot_cuts = [pieces([384, 384])] * (PASSES - 1) + [pieces([384, 256, 128])]
-    out_cuts = pieces([512, 256])
+    token_cuts = pieces([CHUNK] * (T // CHUNK))
+    last_cuts = pieces([384, 256, 128])
+    TURNED = 512
 
     with ExitStack() as ctx:
         lists = ctx.enter_context(tc.tile_pool(name="lists", bufs=1))
@@ -47,45 +52,55 @@ def tile_moe_ecr_lin_relu2_kernel(tc, xT, w_words, w_scales, b, gate, offs, pos1
         slot_tokens = lists.tile([P, SLOTS // LIST_COL], U16, name="slot_tokens")
         token_slots = [lists.tile([P, T // LIST_COL], U16, name=f"token_slots{r}") for r in range(3)]
 
-        token_scales = [keep.tile([P, T], U8, name=f"token_scales{a}", align_bytes=64) for a in range(PASSES)]
-        token_codes = [keep.tile([P, T], U32, name=f"token_codes{a}", align_bytes=64) for a in range(PASSES)]
+        pair_planes = [keep.tile([P, WINDOW], U8, name=f"pair_planes{h}", tag=f"planes{h}", align_bytes=64) for h in range(2)]
+        last_plane = keep.tile([P, T], U8, name="last_plane", align_bytes=64)
+        token_codes = [keep.tile([P, WINDOW], U32, name=f"token_codes{a}", tag=f"codes{a}", align_bytes=64) for a in range(PASSES)]
+        moved_planes = [keep.tile([P, SLOTS], U8, name=f"moved_plane{h}", align_bytes=64) for h in range(2)]
         weight_scales = keep.tile([P, E * PASSES * N], U8, name="weight_scales", align_bytes=64)
         y = keep.tile([P, SLOTS + PAD], F32, name="y")
+        for plane in pair_planes:
+            nc.vector.memset(plane[:].bitcast(I32), 0)
         for a in range(PASSES):
-            nc.vector.memset(token_scales[a][:].bitcast(I32), 0)
+            nc.vector.memset(token_codes[a][:, T:], 0)
         nc.vector.memset(weight_scales[:].bitcast(I32), 0)
+        nc.vector.memset(last_plane[:].bitcast(I32), 0)
+        for plane in moved_planes:
+            nc.vector.memset(plane[:].bitcast(I32), 0)
         nc.vector.memset(y[:, SLOTS:], 0.0)
+        identity = keep.tile([P, P], F32, name="identity")
+        make_identity(nc, identity[:])
 
         raw = {}
         for a in range(PASSES):
             rows = xT[a * K_PASS:(a + 1) * K_PASS, :].rearrange("(p j) t -> p j t", j=PACK)
-            for t0, t1 in token_cuts[a]:
+            for t0, t1 in token_cuts:
                 raw[a, t0] = keep.tile([P, PACK, t1 - t0], F32, name=f"raw{a}_{t0}")
                 nc.sync.dma_start(out=raw[a, t0][:], in_=rows[:, :, t0:t1])
             if a == 0:
                 nc.sync.dma_start(slot_tokens[:], offs)
+            if a == 1:
+                for tile, src in zip(token_slots, (pos1, pos2, pos3)):
+                    nc.sync.dma_start(tile[:], src)
+        bias = keep.tile([P, E], F32, name="bias")
+        nc.scalar.dma_start(out=bias[:], in_=b)
         scale_rows = w_scales.bitcast(I32).rearrange("e a (q r) n -> r q (e a) n", r=4)
         for r in range(4):
             nc.sync.dma_start(
                 out=weight_scales[r:P:32, :].bitcast(I32).rearrange("q (g n) -> q g n", g=E * PASSES), in_=scale_rows[r])
-        weight_codes = []
-        for a in range(PASSES):
-            wt = keep.tile([P, E * 2 * N], U8, name=f"weight_codes{a}", align_bytes=64)
-            nc.sync.dma_start(out=wt[:].bitcast(I32).rearrange("p (e c) -> p e c", e=E),
+
+        def load_weights(dst, a):
+            nc.sync.dma_start(out=dst.bitcast(I32).rearrange("p (e c) -> p e c", e=E),
                               in_=w_words.bitcast(I32)[:, a].rearrange("e p c -> p e c"))
-            weight_codes.append(wt)
-        bias = keep.tile([P, E], F32, name="bias")
-        nc.sync.dma_start(out=bias[:], in_=b)
-        for tile, src in zip(token_slots, (pos1, pos2, pos3)):
-            nc.sync.dma_start(tile[:], src)
-        gates = [keep.tile([P, T], F32, name=f"gate{r}") for r in range(3)]
-        for r in range(3):
-            nc.sync.dma_start(out=gates[r][:], in_=gate[r])
 
-        sums = [psum.tile([P, C], F32, name=f"sums{e}") for e in range(E)]
+        EARLY = 2
+        weight_codes = []
+        for a in range(EARLY):
+            early_weights = keep.tile([P, E * 2 * N], U8, name=f"early_weights{a}", align_bytes=64)
+            load_weights(early_weights[:], a)
+            weight_codes.append(early_weights[:])
 
-        for a in range(PASSES):
-            for t0, t1 in token_cuts[a]:
+        def quantise(a, plane):
+            for t0, t1 in token_cuts:
                 grouped = keep.tile([P, t1 - t0, PACK], BF16, name=f"grouped{a}_{t0}", align_bytes=64)
                 dst = grouped[:].rearrange("p (c i) j -> p c j i", i=4)
                 src = raw[a, t0][:].rearrange("p j (c i) -> p c j i", i=4)
@@ -93,38 +108,87 @@ def tile_moe_ecr_lin_relu2_kernel(tc, xT, w_words, w_scales, b, gate, offs, pos1
                     nc.vector.tensor_copy(out=dst, in_=src)
                 else:
                     nc.scalar.activation(out=dst, in_=src, func=ACT.Copy)
-                nc.vector.quantize_mx(out=token_codes[a][:, t0:t1].bitcast(FP8X4), scales=token_scales[a][:, t0:t1],
+                nc.vector.quantize_mx(out=token_codes[a][:, t0:t1].bitcast(FP8X4), scales=plane[:, t0:t1],
                                       in_=grouped[:].rearrange("p t j -> p (t j)"))
-            for s0, s1 in slot_cuts[a]:
-                picks = slot_tokens[:, s0 // LIST_COL:s1 // LIST_COL]
-                codes = keep.tile([P, s1 - s0], U32, name=f"slot_codes{a}_{s0}", align_bytes=64)
-                scales = keep.tile([P, s1 - s0], U8, name=f"slot_scales{a}_{s0}", align_bytes=64)
-                nc.vector.tensor_copy(codes[:], token_codes[a][:].indirect(picks))
-                nc.vector.tensor_copy(scales[:], token_scales[a][:].indirect(picks))
-                for e in range(s0 // C, s1 // C):
-                    cols = slice(e * C - s0, (e + 1) * C - s0)
-                    g = e * PASSES + a
-                    nc.tensor.matmul_mx(
-                        out=sums[e][:],
-                        lhsT=weight_codes[a][:, e * 2 * N:(e + 1) * 2 * N].bitcast(FP4X4),
-                        lhsT_scale=weight_scales[:, g * N:(g + 1) * N],
-                        rhs=codes[:, cols].bitcast(FP8X4),
-                        rhs_scale=scales[:, cols],
-                        start=(a == 0), stop=(a == PASSES - 1))
 
-        for s0, s1 in slot_cuts[-1]:
+        slot_codes = [keep.tile([P, SLOTS], U32, name=f"slot_codes{a}", align_bytes=64) for a in range(PASSES)]
+        slot_planes = [keep.tile([P, SLOTS], U8, name=f"slot_planes{h}", align_bytes=64) for h in range(2)]
+
+        def gather_codes(a):
+            nc.vector.tensor_copy(slot_codes[a][:], token_codes[a][:].indirect(slot_tokens[:]))
+
+        for h in range(2):
+            quantise(2 * h, pair_planes[h][:])
+            gather_codes(2 * h)
+            quantise(2 * h + 1, pair_planes[h][4:P, :])
+            nc.vector.tensor_copy(slot_planes[h][:], pair_planes[h][:].indirect(slot_tokens[:]))
+            nc.sync.dma_start(out=moved_planes[h][0:MOVED_ROWS, :].bitcast(I32),
+                              in_=slot_planes[h][4:4 + MOVED_ROWS, :].bitcast(I32))
+            gather_codes(2 * h + 1)
+
+        late_weights = keep.tile([P, (PASSES - EARLY) * E * 2 * N], U8, name="late_weights", tag="planes1", align_bytes=64)
+        for a in range(EARLY, PASSES):
+            weight_codes.append(late_weights[:, (a - EARLY) * E * 2 * N:(a - EARLY + 1) * E * 2 * N])
+            load_weights(weight_codes[a], a)
+        gates = keep.tile([P, 3 * T], F32, name="gates", tag="codes3", align_bytes=64)
+        for r in range(3):
+            nc.sync.dma_start(out=gates[:, r * T:(r + 1) * T], in_=gate[r])
+
+        sums = [psum.tile([P, C], F32, name=f"sums{e}", tag=f"bank{e}") for e in range(E)]
+
+        def multiply(a, e, scales):
+            g = e * PASSES + a
+            nc.tensor.matmul_mx(
+                out=sums[e][:],
+                lhsT=weight_codes[a][:, e * 2 * N:(e + 1) * 2 * N].bitcast(FP4X4),
+                lhsT_scale=weight_scales[:, g * N:(g + 1) * N],
+                rhs=slot_codes[a][:, e * C:(e + 1) * C].bitcast(FP8X4),
+                rhs_scale=scales,
+                start=(a == 0), stop=(a == LAST))
+
+        for a, plane in enumerate([slot_planes[0], moved_planes[0], slot_planes[1], moved_planes[1]]):
+            for e in range(E):
+                multiply(a, e, plane[:, e * C:(e + 1) * C])
+
+        quantise(LAST, last_plane[:])
+        for s0, s1 in last_cuts:
+            picks = slot_tokens[:, s0 // LIST_COL:s1 // LIST_COL]
+            scales = keep.tile([P, s1 - s0], U8, name=f"slot_scales{s0}", align_bytes=64)
+            nc.vector.tensor_copy(slot_codes[LAST][:, s0:s1], token_codes[LAST][:].indirect(picks))
+            nc.vector.tensor_copy(scales[:], last_plane[:].indirect(picks))
             clipped = keep.tile([P, s1 - s0], F32, name=f"clipped{s0}")
             for e in range(s0 // C, s1 // C):
-                nc.scalar.activation(out=clipped[:, e * C - s0:(e + 1) * C - s0], in_=sums[e][:], func=ACT.Relu, bias=bias[:, e:e + 1])
+                cols = slice(e * C - s0, (e + 1) * C - s0)
+                multiply(LAST, e, scales[:, cols])
+                nc.scalar.activation(out=clipped[:, cols], in_=sums[e][:], func=ACT.Relu, bias=bias[:, e:e + 1])
             nc.scalar.activation(out=y[:, s0:s1], in_=clipped[:], func=ACT.Square)
 
-        for t0, t1 in out_cuts:
+        def gated_terms(t0, t1):
             terms = [keep.tile([P, t1 - t0], F32, name=f"term{r}_{t0}") for r in range(3)]
             for r in range(3):
                 nc.vector.tensor_tensor(terms[r][:], y[:].indirect(token_slots[r][:, t0 // LIST_COL:t1 // LIST_COL]),
-                                        gates[r][:, t0:t1], ALU.mult)
-            two = keep.tile([P, t1 - t0], F32, name=f"two{t0}")
-            total = keep.tile([P, t1 - t0], F32, name=f"total{t0}")
-            nc.vector.tensor_tensor(two[:], terms[0][:], terms[1][:], ALU.add)
-            nc.vector.tensor_tensor(total[:], two[:], terms[2][:], ALU.add)
-            nc.sync.dma_start(out=out[:, t0:t1], in_=total[:])
+                                        gates[:, r * T + t0:r * T + t1], ALU.mult)
+            return terms
+
+        terms = gated_terms(0, TURNED)
+        blocks = TURNED // P
+        turned_sums = [psum.tile([P, P], F32, name=f"turned_sums{j}", tag=f"bank{j}") for j in range(blocks)]
+        for r in range(3):
+            for j in range(blocks):
+                nc.tensor.matmul(turned_sums[j][:], terms[r][:, j * P:(j + 1) * P], identity[:], is_transpose=True,
+                                 start=(r == 0), stop=(r == 2))
+        turned = keep.tile([P, TURNED], F32, name="turned")
+        upright = psum.tile([P, TURNED], F32, name="upright")
+        for j in range(blocks):
+            nc.scalar.copy(turned[:, j * P:(j + 1) * P], turned_sums[j][:])
+            nc.tensor.transpose(upright[:, j * P:(j + 1) * P], turned[:, j * P:(j + 1) * P], identity[:])
+        first_total = keep.tile([P, TURNED], F32, name="first_total")
+        nc.scalar.copy(first_total[:], upright[:])
+        nc.sync.dma_start(out=out[:, 0:TURNED], in_=first_total[:])
+
+        terms = gated_terms(TURNED, T)
+        two = keep.tile([P, T - TURNED], F32, name="two")
+        total = keep.tile([P, T - TURNED], F32, name="total")
+        nc.vector.tensor_tensor(two[:], terms[0][:], terms[1][:], ALU.add)
+        nc.vector.tensor_tensor(total[:], two[:], terms[2][:], ALU.add)
+        nc.sync.dma_start(out=out[:, TURNED:T], in_=total[:])

@@ -23,11 +23,14 @@ P = 128
 PACK = 4
 K_PASS = P * PACK
 PASSES = K // K_PASS
+SHARED = 4
 LAST = PASSES - 1
 LIST_COL = 16
 WINDOW = 1024
 MOVED_ROWS = 112
 CHUNK = 256
+EARLY = 4
+TURNED = 512
 
 
 def pieces(widths):
@@ -42,7 +45,8 @@ def tile_moe_ecr_lin_relu2_kernel(tc, xT, w_words, w_scales, b, gate, offs, pos1
     nc = tc.nc
     token_cuts = pieces([CHUNK] * (T // CHUNK))
     last_cuts = pieces([384, 256, 128])
-    TURNED = 512
+    out_cuts = pieces([TURNED, T - TURNED])
+    vector_tokens = [448, 288, 160, 160, 0]
 
     with ExitStack() as ctx:
         lists = ctx.enter_context(tc.tile_pool(name="lists", bufs=1))
@@ -52,17 +56,16 @@ def tile_moe_ecr_lin_relu2_kernel(tc, xT, w_words, w_scales, b, gate, offs, pos1
         slot_tokens = lists.tile([P, SLOTS // LIST_COL], U16, name="slot_tokens")
         token_slots = [lists.tile([P, T // LIST_COL], U16, name=f"token_slots{r}") for r in range(3)]
 
-        pair_planes = [keep.tile([P, WINDOW], U8, name=f"pair_planes{h}", tag=f"planes{h}", align_bytes=64) for h in range(2)]
+        shared_planes = keep.tile([P, WINDOW], U8, name="shared_planes", tag="planes_then_weights", align_bytes=64)
         last_plane = keep.tile([P, T], U8, name="last_plane", align_bytes=64)
         token_codes = [keep.tile([P, WINDOW], U32, name=f"token_codes{a}", tag=f"codes{a}", align_bytes=64) for a in range(PASSES)]
-        moved_planes = [keep.tile([P, SLOTS], U8, name=f"moved_plane{h}", align_bytes=64) for h in range(2)]
+        moved_planes = [keep.tile([P, SLOTS], U8, name=f"moved_plane{a}", align_bytes=64) for a in range(1, SHARED)]
         weight_scales = keep.tile([P, E * PASSES * N], U8, name="weight_scales", align_bytes=64)
         y = keep.tile([P, SLOTS + PAD], F32, name="y")
-        for plane in pair_planes:
-            nc.vector.memset(plane[:].bitcast(I32), 0)
+        nc.vector.memset(weight_scales[:].bitcast(I32), 0)
+        nc.vector.memset(shared_planes[:].bitcast(I32), 0)
         for a in range(PASSES):
             nc.vector.memset(token_codes[a][:, T:], 0)
-        nc.vector.memset(weight_scales[:].bitcast(I32), 0)
         nc.vector.memset(last_plane[:].bitcast(I32), 0)
         for plane in moved_planes:
             nc.vector.memset(plane[:].bitcast(I32), 0)
@@ -70,125 +73,135 @@ def tile_moe_ecr_lin_relu2_kernel(tc, xT, w_words, w_scales, b, gate, offs, pos1
         identity = keep.tile([P, P], F32, name="identity")
         make_identity(nc, identity[:])
 
-        raw = {}
+        bias = keep.tile([P, E], F32, name="bias")
+        raw = [keep.tile([P, PACK, T], F32, name=f"raw{a}") for a in range(PASSES)]
         for a in range(PASSES):
-            rows = xT[a * K_PASS:(a + 1) * K_PASS, :].rearrange("(p j) t -> p j t", j=PACK)
-            for t0, t1 in token_cuts:
-                raw[a, t0] = keep.tile([P, PACK, t1 - t0], F32, name=f"raw{a}_{t0}")
-                nc.sync.dma_start(out=raw[a, t0][:], in_=rows[:, :, t0:t1])
+            nc.sync.dma_start(out=raw[a][:], in_=xT[a * K_PASS:(a + 1) * K_PASS, :].rearrange("(p j) t -> p j t", j=PACK))
             if a == 0:
                 nc.sync.dma_start(slot_tokens[:], offs)
-            if a == 1:
+            if a == LAST - 1:
+                nc.sync.dma_start(out=bias[:], in_=b)
                 for tile, src in zip(token_slots, (pos1, pos2, pos3)):
                     nc.sync.dma_start(tile[:], src)
-        bias = keep.tile([P, E], F32, name="bias")
-        nc.scalar.dma_start(out=bias[:], in_=b)
-        scale_rows = w_scales.bitcast(I32).rearrange("e a (q r) n -> r q (e a) n", r=4)
-        for r in range(4):
-            nc.sync.dma_start(
-                out=weight_scales[r:P:32, :].bitcast(I32).rearrange("q (g n) -> q g n", g=E * PASSES), in_=scale_rows[r])
+        nc.sync.dma_start(out=weight_scales[0:16, :].bitcast(I32).rearrange("q (g n) -> q g n", g=E * PASSES),
+                          in_=w_scales.bitcast(I32).rearrange("e a q n -> q (e a) n"))
 
-        def load_weights(dst, a):
-            nc.sync.dma_start(out=dst.bitcast(I32).rearrange("p (e c) -> p e c", e=E),
-                              in_=w_words.bitcast(I32)[:, a].rearrange("e p c -> p e c"))
+        EXPERT_BYTES = PASSES * 2 * N
 
-        EARLY = 2
-        weight_codes = []
-        for a in range(EARLY):
-            early_weights = keep.tile([P, E * 2 * N], U8, name=f"early_weights{a}", align_bytes=64)
-            load_weights(early_weights[:], a)
-            weight_codes.append(early_weights[:])
+        def load_weights(dst, e0, e1):
+            nc.sync.dma_start(out=dst.bitcast(I32).rearrange("p (g c) -> p g c", g=(e1 - e0) * PASSES),
+                              in_=w_words.bitcast(I32)[e0:e1].rearrange("e a p c -> p (e a) c"))
+
+        early_weights = keep.tile([P, EARLY * EXPERT_BYTES], U8, name="early_weights", align_bytes=64)
+        for e0 in range(0, EARLY, 2):
+            load_weights(early_weights[:, e0 * EXPERT_BYTES:(e0 + 2) * EXPERT_BYTES], e0, e0 + 2)
+        for q in range(1, 4):
+            nc.sync.dma_start(out=weight_scales[32 * q:32 * q + 4, :].bitcast(I32), in_=weight_scales[4 * q:4 * q + 4, :].bitcast(I32))
 
         def quantise(a, plane):
+            grouped = keep.tile([P, T, PACK], BF16, name=f"grouped{a}", align_bytes=64)
+            border = T - vector_tokens[a]
             for t0, t1 in token_cuts:
-                grouped = keep.tile([P, t1 - t0, PACK], BF16, name=f"grouped{a}_{t0}", align_bytes=64)
-                dst = grouped[:].rearrange("p (c i) j -> p c j i", i=4)
-                src = raw[a, t0][:].rearrange("p j (c i) -> p c j i", i=4)
-                if a == 0 and t1 == T:
-                    nc.vector.tensor_copy(out=dst, in_=src)
-                else:
-                    nc.scalar.activation(out=dst, in_=src, func=ACT.Copy)
+                for c0, c1, on_scalar in ((t0, min(t1, border), True), (max(t0, border), t1, False)):
+                    if c0 < c1:
+                        dst = grouped[:, c0:c1, :].rearrange("p (c i) j -> p c j i", i=2)
+                        src = raw[a][:, :, c0:c1].rearrange("p j (c i) -> p c j i", i=2)
+                        if on_scalar:
+                            nc.scalar.activation(out=dst, in_=src, func=ACT.Copy)
+                        else:
+                            nc.vector.tensor_copy(out=dst, in_=src)
                 nc.vector.quantize_mx(out=token_codes[a][:, t0:t1].bitcast(FP8X4), scales=plane[:, t0:t1],
-                                      in_=grouped[:].rearrange("p t j -> p (t j)"))
+                                      in_=grouped[:, t0:t1, :].rearrange("p t j -> p (t j)"))
 
         slot_codes = [keep.tile([P, SLOTS], U32, name=f"slot_codes{a}", align_bytes=64) for a in range(PASSES)]
-        slot_planes = [keep.tile([P, SLOTS], U8, name=f"slot_planes{h}", align_bytes=64) for h in range(2)]
+        slot_planes = keep.tile([P, SLOTS], U8, name="slot_planes", align_bytes=64)
 
-        def gather_codes(a):
-            nc.vector.tensor_copy(slot_codes[a][:], token_codes[a][:].indirect(slot_tokens[:]))
-
-        for h in range(2):
-            quantise(2 * h, pair_planes[h][:])
-            gather_codes(2 * h)
-            quantise(2 * h + 1, pair_planes[h][4:P, :])
-            nc.vector.tensor_copy(slot_planes[h][:], pair_planes[h][:].indirect(slot_tokens[:]))
-            nc.sync.dma_start(out=moved_planes[h][0:MOVED_ROWS, :].bitcast(I32),
-                              in_=slot_planes[h][4:4 + MOVED_ROWS, :].bitcast(I32))
-            gather_codes(2 * h + 1)
-
-        late_weights = keep.tile([P, (PASSES - EARLY) * E * 2 * N], U8, name="late_weights", tag="planes1", align_bytes=64)
-        for a in range(EARLY, PASSES):
-            weight_codes.append(late_weights[:, (a - EARLY) * E * 2 * N:(a - EARLY + 1) * E * 2 * N])
-            load_weights(weight_codes[a], a)
-        gates = keep.tile([P, 3 * T], F32, name="gates", tag="codes3", align_bytes=64)
-        for r in range(3):
-            nc.sync.dma_start(out=gates[:, r * T:(r + 1) * T], in_=gate[r])
+        for a in range(SHARED):
+            quantise(a, shared_planes[4 * a:P, :])
+            if a < SHARED - 1:
+                nc.vector.tensor_copy(slot_codes[a][:], token_codes[a][:].indirect(slot_tokens[:]))
+        nc.vector.tensor_copy(slot_planes[:], shared_planes[:].indirect(slot_tokens[:]))
+        late_weights = keep.tile([P, (E - EARLY) * EXPERT_BYTES], U8, name="late_weights", tag="planes_then_weights", align_bytes=64)
+        for m in range(1, SHARED):
+            nc.sync.dma_start(out=moved_planes[m - 1][0:MOVED_ROWS, :].bitcast(I32),
+                              in_=slot_planes[4 * m:4 * m + MOVED_ROWS, :].bitcast(I32))
+            if m <= E - EARLY:
+                load_weights(late_weights[:, (m - 1) * EXPERT_BYTES:m * EXPERT_BYTES], EARLY + m - 1, EARLY + m)
+        nc.vector.tensor_copy(slot_codes[SHARED - 1][:], token_codes[SHARED - 1][:].indirect(slot_tokens[:]))
+        gates = keep.tile([P, 3 * T], F32, name="gates", tag=f"codes{SHARED - 1}", align_bytes=64)
+        for t0, t1 in out_cuts:
+            for r in range(3):
+                nc.sync.dma_start(out=gates[:, r * T + t0:r * T + t1], in_=gate[r, :, t0:t1])
 
         sums = [psum.tile([P, C], F32, name=f"sums{e}", tag=f"bank{e}") for e in range(E)]
 
         def multiply(a, e, scales):
             g = e * PASSES + a
+            weights, at = (early_weights, g * 2 * N) if e < EARLY else (late_weights, (g - EARLY * PASSES) * 2 * N)
             nc.tensor.matmul_mx(
                 out=sums[e][:],
-                lhsT=weight_codes[a][:, e * 2 * N:(e + 1) * 2 * N].bitcast(FP4X4),
+                lhsT=weights[:, at:at + 2 * N].bitcast(FP4X4),
                 lhsT_scale=weight_scales[:, g * N:(g + 1) * N],
                 rhs=slot_codes[a][:, e * C:(e + 1) * C].bitcast(FP8X4),
                 rhs_scale=scales,
                 start=(a == 0), stop=(a == LAST))
 
-        for a, plane in enumerate([slot_planes[0], moved_planes[0], slot_planes[1], moved_planes[1]]):
-            for e in range(E):
-                multiply(a, e, plane[:, e * C:(e + 1) * C])
+        planes = [slot_planes] + moved_planes
+        for a in range(SHARED):
+            for e in range(EARLY):
+                multiply(a, e, planes[a][:, e * C:(e + 1) * C])
 
         quantise(LAST, last_plane[:])
+        nc.vector.tensor_copy(slot_codes[LAST][:], token_codes[LAST][:].indirect(slot_tokens[:]))
+        clipped = keep.tile([P, SLOTS], F32, name="clipped")
         for s0, s1 in last_cuts:
             picks = slot_tokens[:, s0 // LIST_COL:s1 // LIST_COL]
             scales = keep.tile([P, s1 - s0], U8, name=f"slot_scales{s0}", align_bytes=64)
-            nc.vector.tensor_copy(slot_codes[LAST][:, s0:s1], token_codes[LAST][:].indirect(picks))
             nc.vector.tensor_copy(scales[:], last_plane[:].indirect(picks))
-            clipped = keep.tile([P, s1 - s0], F32, name=f"clipped{s0}")
             for e in range(s0 // C, s1 // C):
-                cols = slice(e * C - s0, (e + 1) * C - s0)
-                multiply(LAST, e, scales[:, cols])
-                nc.scalar.activation(out=clipped[:, cols], in_=sums[e][:], func=ACT.Relu, bias=bias[:, e:e + 1])
-            nc.scalar.activation(out=y[:, s0:s1], in_=clipped[:], func=ACT.Square)
+                if e >= EARLY:
+                    for a in range(SHARED):
+                        multiply(a, e, planes[a][:, e * C:(e + 1) * C])
+                multiply(LAST, e, scales[:, e * C - s0:(e + 1) * C - s0])
+                nc.scalar.activation(out=clipped[:, e * C:(e + 1) * C], in_=sums[e][:], func=ACT.Relu, bias=bias[:, e:e + 1])
+        for s0, s1 in last_cuts:
+            nc.vector.tensor_tensor(y[:, s0:s1], clipped[:, s0:s1], clipped[:, s0:s1], ALU.mult)
 
-        def gated_terms(t0, t1):
-            terms = [keep.tile([P, t1 - t0], F32, name=f"term{r}_{t0}") for r in range(3)]
-            for r in range(3):
-                nc.vector.tensor_tensor(terms[r][:], y[:].indirect(token_slots[r][:, t0 // LIST_COL:t1 // LIST_COL]),
-                                        gates[:, r * T + t0:r * T + t1], ALU.mult)
-            return terms
+        terms = [keep.tile([P, T], F32, name=f"term{r}") for r in range(3)]
 
-        terms = gated_terms(0, TURNED)
+        def gated_term(r, t0, t1):
+            nc.vector.tensor_tensor(terms[r][:, t0:t1], y[:].indirect(token_slots[r][:, t0 // LIST_COL:t1 // LIST_COL]),
+                                    gates[:, r * T + t0:r * T + t1], ALU.mult)
+
         blocks = TURNED // P
         turned_sums = [psum.tile([P, P], F32, name=f"turned_sums{j}", tag=f"bank{j}") for j in range(blocks)]
-        for r in range(3):
-            for j in range(blocks):
-                nc.tensor.matmul(turned_sums[j][:], terms[r][:, j * P:(j + 1) * P], identity[:], is_transpose=True,
-                                 start=(r == 0), stop=(r == 2))
-        turned = keep.tile([P, TURNED], F32, name="turned")
-        upright = psum.tile([P, TURNED], F32, name="upright")
-        for j in range(blocks):
-            nc.scalar.copy(turned[:, j * P:(j + 1) * P], turned_sums[j][:])
-            nc.tensor.transpose(upright[:, j * P:(j + 1) * P], turned[:, j * P:(j + 1) * P], identity[:])
-        first_total = keep.tile([P, TURNED], F32, name="first_total")
-        nc.scalar.copy(first_total[:], upright[:])
-        nc.sync.dma_start(out=out[:, 0:TURNED], in_=first_total[:])
 
-        terms = gated_terms(TURNED, T)
+        def add_turned(r, j):
+            nc.tensor.matmul(turned_sums[j][:], terms[r][:, j * P:(j + 1) * P], identity[:], is_transpose=True,
+                             start=(r == 0), stop=(r == 2))
+
+        for r in range(2):
+            gated_term(r, 0, TURNED)
+            for j in range(blocks):
+                add_turned(r, j)
+        turned = keep.tile([P, TURNED], F32, name="turned")
+        total = keep.tile([P, T], F32, name="total")
+        for t0, t1 in pieces([TURNED // 2] * 2):
+            gated_term(2, t0, t1)
+            upright = psum.tile([P, t1 - t0], F32, name=f"upright{t0}")
+            for j in range(t0 // P, t1 // P):
+                add_turned(2, j)
+                nc.scalar.copy(turned[:, j * P:(j + 1) * P], turned_sums[j][:])
+                nc.tensor.transpose(upright[:, j * P - t0:(j + 1) * P - t0], turned[:, j * P:(j + 1) * P], identity[:])
+            nc.scalar.copy(total[:, t0:t1], upright[:])
+            nc.scalar.dma_start(out=out[:, t0:t1], in_=total[:, t0:t1])
+
+        for r in range(3):
+            gated_term(r, TURNED, T)
         two = keep.tile([P, T - TURNED], F32, name="two")
-        total = keep.tile([P, T - TURNED], F32, name="total")
-        nc.vector.tensor_tensor(two[:], terms[0][:], terms[1][:], ALU.add)
-        nc.vector.tensor_tensor(total[:], two[:], terms[2][:], ALU.add)
-        nc.sync.dma_start(out=out[:, TURNED:T], in_=total[:])
+        halves = pieces([(T - TURNED) // 2] * 2)
+        for h0, h1 in halves:
+            nc.vector.tensor_tensor(two[:, h0:h1], terms[0][:, TURNED + h0:TURNED + h1], terms[1][:, TURNED + h0:TURNED + h1], ALU.add)
+        for h0, h1 in halves:
+            nc.vector.tensor_tensor(total[:, TURNED + h0:TURNED + h1], two[:, h0:h1], terms[2][:, TURNED + h0:TURNED + h1], ALU.add)
+        nc.sync.dma_start(out=out[:, TURNED:T], in_=total[:, TURNED:T])

@@ -6,6 +6,7 @@ from concourse.masks import make_identity
 K, T, E, C, N = 2560, 768, 6, 128, 128
 SLOTS = E * C
 PAD = 64
+CHOICES = 3
 FLOPS = 2 * K * N * SLOTS
 
 F32 = mybir.dt.float32
@@ -23,30 +24,33 @@ P = 128
 PACK = 4
 K_PASS = P * PACK
 PASSES = K // K_PASS
-SHARED = 4
 LAST = PASSES - 1
+QUADRANT = 32
+LIVE = 4
+SHARED = 4
 LIST_COL = 16
 WINDOW = 1024
 MOVED_ROWS = 112
 CHUNK = 256
-EARLY = 4
+PASS_BYTES = 2 * N
+EXPERT_BYTES = PASSES * PASS_BYTES
+EARLY = 3
 TURNED = 512
+
+VECTOR_TOKENS = [448, 288, 160, 160, 0]
+LAST_PIECES = [384, 256, 128]
 
 
 def pieces(widths):
-    out, start = [], 0
-    for w in widths:
-        out.append((start, start + w))
-        start = start + w
-    return out
+    ranges, start = [], 0
+    for width in widths:
+        ranges.append((start, start + width))
+        start = start + width
+    return ranges
 
 
 def tile_moe_ecr_lin_relu2_kernel(tc, xT, w_words, w_scales, b, gate, offs, pos1, pos2, pos3, out):
     nc = tc.nc
-    token_cuts = pieces([CHUNK] * (T // CHUNK))
-    last_cuts = pieces([384, 256, 128])
-    out_cuts = pieces([TURNED, T - TURNED])
-    vector_tokens = [448, 288, 160, 160, 0]
 
     with ExitStack() as ctx:
         lists = ctx.enter_context(tc.tile_pool(name="lists", bufs=1))
@@ -54,7 +58,7 @@ def tile_moe_ecr_lin_relu2_kernel(tc, xT, w_words, w_scales, b, gate, offs, pos1
         psum = ctx.enter_context(tc.psum_pool(name="psum", bufs=1))
 
         slot_tokens = lists.tile([P, SLOTS // LIST_COL], U16, name="slot_tokens")
-        token_slots = [lists.tile([P, T // LIST_COL], U16, name=f"token_slots{r}") for r in range(3)]
+        token_slots = [lists.tile([P, T // LIST_COL], U16, name=f"token_slots{r}") for r in range(CHOICES)]
 
         shared_planes = keep.tile([P, WINDOW], U8, name="shared_planes", tag="planes_then_weights", align_bytes=64)
         last_plane = keep.tile([P, T], U8, name="last_plane", align_bytes=64)
@@ -83,25 +87,24 @@ def tile_moe_ecr_lin_relu2_kernel(tc, xT, w_words, w_scales, b, gate, offs, pos1
                 nc.sync.dma_start(out=bias[:], in_=b)
                 for tile, src in zip(token_slots, (pos1, pos2, pos3)):
                     nc.sync.dma_start(tile[:], src)
-        nc.sync.dma_start(out=weight_scales[0:16, :].bitcast(I32).rearrange("q (g n) -> q g n", g=E * PASSES),
-                          in_=w_scales.bitcast(I32).rearrange("e a q n -> q (e a) n"))
 
-        EXPERT_BYTES = PASSES * 2 * N
+        nc.sync.dma_start(out=weight_scales[0:PACK * LIVE, :].bitcast(I32).rearrange("q (g n) -> q g n", g=E * PASSES),
+                          in_=w_scales.bitcast(I32).rearrange("e a q n -> q (e a) n"))
 
         def load_weights(dst, e0, e1):
             nc.sync.dma_start(out=dst.bitcast(I32).rearrange("p (g c) -> p g c", g=(e1 - e0) * PASSES),
                               in_=w_words.bitcast(I32)[e0:e1].rearrange("e a p c -> p (e a) c"))
 
         early_weights = keep.tile([P, EARLY * EXPERT_BYTES], U8, name="early_weights", align_bytes=64)
-        for e0 in range(0, EARLY, 2):
-            load_weights(early_weights[:, e0 * EXPERT_BYTES:(e0 + 2) * EXPERT_BYTES], e0, e0 + 2)
-        for q in range(1, 4):
-            nc.sync.dma_start(out=weight_scales[32 * q:32 * q + 4, :].bitcast(I32), in_=weight_scales[4 * q:4 * q + 4, :].bitcast(I32))
+        load_weights(early_weights[:], 0, EARLY)
+        for quad in range(1, P // QUADRANT):
+            nc.sync.dma_start(out=weight_scales[QUADRANT * quad:QUADRANT * quad + LIVE, :].bitcast(I32),
+                              in_=weight_scales[LIVE * quad:LIVE * (quad + 1), :].bitcast(I32))
 
         def quantise(a, plane):
             grouped = keep.tile([P, T, PACK], BF16, name=f"grouped{a}", align_bytes=64)
-            border = T - vector_tokens[a]
-            for t0, t1 in token_cuts:
+            border = T - VECTOR_TOKENS[a]
+            for t0, t1 in pieces([CHUNK] * (T // CHUNK)):
                 for c0, c1, on_scalar in ((t0, min(t1, border), True), (max(t0, border), t1, False)):
                     if c0 < c1:
                         dst = grouped[:, c0:c1, :].rearrange("p (c i) j -> p c j i", i=2)
@@ -116,58 +119,61 @@ def tile_moe_ecr_lin_relu2_kernel(tc, xT, w_words, w_scales, b, gate, offs, pos1
         slot_codes = [keep.tile([P, SLOTS], U32, name=f"slot_codes{a}", align_bytes=64) for a in range(PASSES)]
         slot_planes = keep.tile([P, SLOTS], U8, name="slot_planes", align_bytes=64)
 
+        def gather_codes(a):
+            nc.vector.tensor_copy(slot_codes[a][:], token_codes[a][:].indirect(slot_tokens[:]))
+
         for a in range(SHARED):
-            quantise(a, shared_planes[4 * a:P, :])
+            quantise(a, shared_planes[LIVE * a:P, :])
             if a < SHARED - 1:
-                nc.vector.tensor_copy(slot_codes[a][:], token_codes[a][:].indirect(slot_tokens[:]))
+                gather_codes(a)
+
         nc.vector.tensor_copy(slot_planes[:], shared_planes[:].indirect(slot_tokens[:]))
         late_weights = keep.tile([P, (E - EARLY) * EXPERT_BYTES], U8, name="late_weights", tag="planes_then_weights", align_bytes=64)
-        for m in range(1, SHARED):
-            nc.sync.dma_start(out=moved_planes[m - 1][0:MOVED_ROWS, :].bitcast(I32),
-                              in_=slot_planes[4 * m:4 * m + MOVED_ROWS, :].bitcast(I32))
-            if m <= E - EARLY:
-                load_weights(late_weights[:, (m - 1) * EXPERT_BYTES:m * EXPERT_BYTES], EARLY + m - 1, EARLY + m)
-        nc.vector.tensor_copy(slot_codes[SHARED - 1][:], token_codes[SHARED - 1][:].indirect(slot_tokens[:]))
-        gates = keep.tile([P, 3 * T], F32, name="gates", tag=f"codes{SHARED - 1}", align_bytes=64)
-        for t0, t1 in out_cuts:
-            for r in range(3):
+        for a in range(1, SHARED):
+            nc.sync.dma_start(out=moved_planes[a - 1][0:MOVED_ROWS, :].bitcast(I32),
+                              in_=slot_planes[LIVE * a:LIVE * a + MOVED_ROWS, :].bitcast(I32))
+            load_weights(late_weights[:, (a - 1) * EXPERT_BYTES:a * EXPERT_BYTES], EARLY + a - 1, EARLY + a)
+        gather_codes(SHARED - 1)
+
+        gates = keep.tile([P, CHOICES * T], F32, name="gates", tag=f"codes{SHARED - 1}", align_bytes=64)
+        for t0, t1 in pieces([TURNED, T - TURNED]):
+            for r in range(CHOICES):
                 nc.sync.dma_start(out=gates[:, r * T + t0:r * T + t1], in_=gate[r, :, t0:t1])
 
         sums = [psum.tile([P, C], F32, name=f"sums{e}", tag=f"bank{e}") for e in range(E)]
 
         def multiply(a, e, scales):
             g = e * PASSES + a
-            weights, at = (early_weights, g * 2 * N) if e < EARLY else (late_weights, (g - EARLY * PASSES) * 2 * N)
+            weights, at = (early_weights, g * PASS_BYTES) if e < EARLY else (late_weights, (g - EARLY * PASSES) * PASS_BYTES)
             nc.tensor.matmul_mx(
                 out=sums[e][:],
-                lhsT=weights[:, at:at + 2 * N].bitcast(FP4X4),
+                lhsT=weights[:, at:at + PASS_BYTES].bitcast(FP4X4),
                 lhsT_scale=weight_scales[:, g * N:(g + 1) * N],
                 rhs=slot_codes[a][:, e * C:(e + 1) * C].bitcast(FP8X4),
                 rhs_scale=scales,
                 start=(a == 0), stop=(a == LAST))
 
-        planes = [slot_planes] + moved_planes
+        pass_planes = [slot_planes] + moved_planes
         for a in range(SHARED):
             for e in range(EARLY):
-                multiply(a, e, planes[a][:, e * C:(e + 1) * C])
+                multiply(a, e, pass_planes[a][:, e * C:(e + 1) * C])
 
         quantise(LAST, last_plane[:])
-        nc.vector.tensor_copy(slot_codes[LAST][:], token_codes[LAST][:].indirect(slot_tokens[:]))
+        gather_codes(LAST)
         clipped = keep.tile([P, SLOTS], F32, name="clipped")
-        for s0, s1 in last_cuts:
-            picks = slot_tokens[:, s0 // LIST_COL:s1 // LIST_COL]
-            scales = keep.tile([P, s1 - s0], U8, name=f"slot_scales{s0}", align_bytes=64)
-            nc.vector.tensor_copy(scales[:], last_plane[:].indirect(picks))
+        for s0, s1 in pieces(LAST_PIECES):
+            last_scales = keep.tile([P, s1 - s0], U8, name=f"slot_scales{s0}", align_bytes=64)
+            nc.vector.tensor_copy(last_scales[:], last_plane[:].indirect(slot_tokens[:, s0 // LIST_COL:s1 // LIST_COL]))
             for e in range(s0 // C, s1 // C):
                 if e >= EARLY:
                     for a in range(SHARED):
-                        multiply(a, e, planes[a][:, e * C:(e + 1) * C])
-                multiply(LAST, e, scales[:, e * C - s0:(e + 1) * C - s0])
+                        multiply(a, e, pass_planes[a][:, e * C:(e + 1) * C])
+                multiply(LAST, e, last_scales[:, e * C - s0:(e + 1) * C - s0])
                 nc.scalar.activation(out=clipped[:, e * C:(e + 1) * C], in_=sums[e][:], func=ACT.Relu, bias=bias[:, e:e + 1])
-        for s0, s1 in last_cuts:
+        for s0, s1 in pieces(LAST_PIECES):
             nc.vector.tensor_tensor(y[:, s0:s1], clipped[:, s0:s1], clipped[:, s0:s1], ALU.mult)
 
-        terms = [keep.tile([P, T], F32, name=f"term{r}") for r in range(3)]
+        terms = [keep.tile([P, T], F32, name=f"term{r}") for r in range(CHOICES)]
 
         def gated_term(r, t0, t1):
             nc.vector.tensor_tensor(terms[r][:, t0:t1], y[:].indirect(token_slots[r][:, t0 // LIST_COL:t1 // LIST_COL]),
@@ -178,30 +184,30 @@ def tile_moe_ecr_lin_relu2_kernel(tc, xT, w_words, w_scales, b, gate, offs, pos1
 
         def add_turned(r, j):
             nc.tensor.matmul(turned_sums[j][:], terms[r][:, j * P:(j + 1) * P], identity[:], is_transpose=True,
-                             start=(r == 0), stop=(r == 2))
+                             start=(r == 0), stop=(r == CHOICES - 1))
 
-        for r in range(2):
+        for r in range(CHOICES - 1):
             gated_term(r, 0, TURNED)
             for j in range(blocks):
                 add_turned(r, j)
         turned = keep.tile([P, TURNED], F32, name="turned")
         total = keep.tile([P, T], F32, name="total")
         for t0, t1 in pieces([TURNED // 2] * 2):
-            gated_term(2, t0, t1)
+            gated_term(CHOICES - 1, t0, t1)
             upright = psum.tile([P, t1 - t0], F32, name=f"upright{t0}")
             for j in range(t0 // P, t1 // P):
-                add_turned(2, j)
+                add_turned(CHOICES - 1, j)
                 nc.scalar.copy(turned[:, j * P:(j + 1) * P], turned_sums[j][:])
                 nc.tensor.transpose(upright[:, j * P - t0:(j + 1) * P - t0], turned[:, j * P:(j + 1) * P], identity[:])
             nc.scalar.copy(total[:, t0:t1], upright[:])
             nc.scalar.dma_start(out=out[:, t0:t1], in_=total[:, t0:t1])
 
-        for r in range(3):
+        for r in range(CHOICES):
             gated_term(r, TURNED, T)
-        two = keep.tile([P, T - TURNED], F32, name="two")
+        two_terms = keep.tile([P, T - TURNED], F32, name="two")
         halves = pieces([(T - TURNED) // 2] * 2)
         for h0, h1 in halves:
-            nc.vector.tensor_tensor(two[:, h0:h1], terms[0][:, TURNED + h0:TURNED + h1], terms[1][:, TURNED + h0:TURNED + h1], ALU.add)
+            nc.vector.tensor_tensor(two_terms[:, h0:h1], terms[0][:, TURNED + h0:TURNED + h1], terms[1][:, TURNED + h0:TURNED + h1], ALU.add)
         for h0, h1 in halves:
-            nc.vector.tensor_tensor(total[:, TURNED + h0:TURNED + h1], two[:, h0:h1], terms[2][:, TURNED + h0:TURNED + h1], ALU.add)
+            nc.vector.tensor_tensor(total[:, TURNED + h0:TURNED + h1], two_terms[:, h0:h1], terms[2][:, TURNED + h0:TURNED + h1], ALU.add)
         nc.sync.dma_start(out=out[:, TURNED:T], in_=total[:, TURNED:T])

@@ -35,7 +35,10 @@ CHUNK = 256
 PASS_BYTES = 2 * N
 EXPERT_BYTES = PASSES * PASS_BYTES
 EARLY = 3
-TURNED = 512
+UPRIGHT_BLOCKS = [256, 256]
+UPRIGHT = sum(UPRIGHT_BLOCKS)
+TURNED = T - UPRIGHT
+TURNED_BLOCKS = TURNED // P
 
 VECTOR_TOKENS = [448, 288, 160, 160, 0]
 LAST_PIECES = [384, 256, 128]
@@ -66,7 +69,9 @@ def tile_moe_ecr_lin_relu2_kernel(tc, xT, w_words, w_scales, b, gate, offs, pos1
         moved_planes = [keep.tile([P, SLOTS], U8, name=f"moved_plane{a}", align_bytes=64) for a in range(1, SHARED)]
         weight_scales = keep.tile([P, E * PASSES * N], U8, name="weight_scales", align_bytes=64)
         y = keep.tile([P, SLOTS + PAD], F32, name="y")
+        gate_rows = keep.tile([P, TURNED], F32, name="gate_rows")
         nc.vector.memset(weight_scales[:].bitcast(I32), 0)
+        nc.vector.memset(gate_rows[:], 0.0)
         nc.vector.memset(shared_planes[:].bitcast(I32), 0)
         for a in range(PASSES):
             nc.vector.memset(token_codes[a][:, T:], 0)
@@ -87,6 +92,7 @@ def tile_moe_ecr_lin_relu2_kernel(tc, xT, w_words, w_scales, b, gate, offs, pos1
                 nc.sync.dma_start(out=bias[:], in_=b)
                 for tile, src in zip(token_slots, (pos1, pos2, pos3)):
                     nc.sync.dma_start(tile[:], src)
+                nc.sync.dma_start(out=gate_rows[0:CHOICES, :], in_=gate[:, 0, UPRIGHT:T])
 
         nc.sync.dma_start(out=weight_scales[0:PACK * LIVE, :].bitcast(I32).rearrange("q (g n) -> q g n", g=E * PASSES),
                           in_=w_scales.bitcast(I32).rearrange("e a q n -> q (e a) n"))
@@ -135,10 +141,9 @@ def tile_moe_ecr_lin_relu2_kernel(tc, xT, w_words, w_scales, b, gate, offs, pos1
             load_weights(late_weights[:, (a - 1) * EXPERT_BYTES:a * EXPERT_BYTES], EARLY + a - 1, EARLY + a)
         gather_codes(SHARED - 1)
 
-        gates = keep.tile([P, CHOICES * T], F32, name="gates", tag=f"codes{SHARED - 1}", align_bytes=64)
-        for t0, t1 in pieces([TURNED, T - TURNED]):
-            for r in range(CHOICES):
-                nc.sync.dma_start(out=gates[:, r * T + t0:r * T + t1], in_=gate[r, :, t0:t1])
+        gates = keep.tile([P, CHOICES, UPRIGHT], F32, name="gates", tag=f"codes{SHARED - 1}", align_bytes=64)
+        for r in range(CHOICES):
+            nc.sync.dma_start(out=gates[:, r, :], in_=gate[r, :, 0:UPRIGHT])
 
         sums = [psum.tile([P, C], F32, name=f"sums{e}", tag=f"bank{e}") for e in range(E)]
 
@@ -173,41 +178,41 @@ def tile_moe_ecr_lin_relu2_kernel(tc, xT, w_words, w_scales, b, gate, offs, pos1
         for s0, s1 in pieces(LAST_PIECES):
             nc.vector.tensor_tensor(y[:, s0:s1], clipped[:, s0:s1], clipped[:, s0:s1], ALU.mult)
 
-        terms = [keep.tile([P, T], F32, name=f"term{r}") for r in range(CHOICES)]
+        gate_turned = psum.tile([P, TURNED_BLOCKS, P], F32, name="gate_turned", tag=f"bank{E - 1}")
+        for j in range(TURNED_BLOCKS):
+            nc.tensor.transpose(gate_turned[:, j, :], gate_rows[:, j * P:(j + 1) * P], identity[:])
+        gate_columns = keep.tile([P, TURNED_BLOCKS, CHOICES], F32, name="gate_columns")
+        nc.scalar.copy(gate_columns[:], gate_turned[:, :, 0:CHOICES])
 
-        def gated_term(r, t0, t1):
-            nc.vector.tensor_tensor(terms[r][:, t0:t1], y[:].indirect(token_slots[r][:, t0 // LIST_COL:t1 // LIST_COL]),
-                                    gates[:, r * T + t0:r * T + t1], ALU.mult)
+        def results(r, t0, t1):
+            return y[:].indirect(token_slots[r][:, t0 // LIST_COL:t1 // LIST_COL])
 
-        blocks = TURNED // P
-        turned_sums = [psum.tile([P, P], F32, name=f"turned_sums{j}", tag=f"bank{j}") for j in range(blocks)]
-
-        def add_turned(r, j):
-            nc.tensor.matmul(turned_sums[j][:], terms[r][:, j * P:(j + 1) * P], identity[:], is_transpose=True,
-                             start=(r == 0), stop=(r == CHOICES - 1))
-
-        for r in range(CHOICES - 1):
-            gated_term(r, 0, TURNED)
-            for j in range(blocks):
-                add_turned(r, j)
-        turned = keep.tile([P, TURNED], F32, name="turned")
-        total = keep.tile([P, T], F32, name="total")
-        for t0, t1 in pieces([TURNED // 2] * 2):
-            gated_term(CHOICES - 1, t0, t1)
-            upright = psum.tile([P, t1 - t0], F32, name=f"upright{t0}")
-            for j in range(t0 // P, t1 // P):
-                add_turned(CHOICES - 1, j)
-                nc.scalar.copy(turned[:, j * P:(j + 1) * P], turned_sums[j][:])
-                nc.tensor.transpose(upright[:, j * P - t0:(j + 1) * P - t0], turned[:, j * P:(j + 1) * P], identity[:])
-            nc.scalar.copy(total[:, t0:t1], upright[:])
-            nc.scalar.dma_start(out=out[:, t0:t1], in_=total[:, t0:t1])
-
+        blocks = pieces([P] * TURNED_BLOCKS)
+        summed = [psum.tile([P, P], F32, name=f"summed{j}", tag=f"bank{CHOICES + j}") for j in range(TURNED_BLOCKS)]
+        gated = keep.tile([P, CHOICES, TURNED], F32, name="gated")
         for r in range(CHOICES):
-            gated_term(r, TURNED, T)
-        two_terms = keep.tile([P, T - TURNED], F32, name="two")
-        halves = pieces([(T - TURNED) // 2] * 2)
-        for h0, h1 in halves:
-            nc.vector.tensor_tensor(two_terms[:, h0:h1], terms[0][:, TURNED + h0:TURNED + h1], terms[1][:, TURNED + h0:TURNED + h1], ALU.add)
-        for h0, h1 in halves:
-            nc.vector.tensor_tensor(total[:, TURNED + h0:TURNED + h1], two_terms[:, h0:h1], terms[2][:, TURNED + h0:TURNED + h1], ALU.add)
-        nc.sync.dma_start(out=out[:, TURNED:T], in_=total[:, TURNED:T])
+            fetched = keep.tile([P, TURNED], F32, name=f"fetched{r}")
+            nc.scalar.activation(out=fetched[:], in_=results(r, UPRIGHT, T), func=ACT.Copy)
+            turned = psum.tile([P, TURNED], F32, name=f"turned{r}", tag=f"bank{r}")
+            for t0, t1 in blocks:
+                nc.tensor.transpose(turned[:, t0:t1], fetched[:, t0:t1], identity[:])
+            for j, (t0, t1) in enumerate(blocks):
+                nc.scalar.activation(out=gated[:, r, t0:t1], in_=turned[:, t0:t1], func=ACT.Copy,
+                                     scale=gate_columns[:, j, r:r + 1])
+                nc.tensor.matmul(summed[j][:], gated[:, r, t0:t1], identity[:], is_transpose=True,
+                                 start=(r == 0), stop=(r == CHOICES - 1))
+        turned_total = keep.tile([P, TURNED], F32, name="turned_total")
+        for j, (t0, t1) in enumerate(blocks):
+            nc.scalar.copy(turned_total[:, t0:t1], summed[j][:])
+        nc.scalar.dma_start(out=out[:, UPRIGHT:T], in_=turned_total[:])
+
+        terms = [keep.tile([P, UPRIGHT], F32, name=f"term{r}") for r in range(CHOICES)]
+        for r in range(CHOICES):
+            nc.vector.tensor_tensor(terms[r][:], results(r, 0, UPRIGHT), gates[:, r, :], ALU.mult)
+        two_terms = keep.tile([P, UPRIGHT], F32, name="two_terms")
+        total = keep.tile([P, UPRIGHT], F32, name="total")
+        for t0, t1 in pieces(UPRIGHT_BLOCKS):
+            nc.vector.tensor_tensor(two_terms[:, t0:t1], terms[0][:, t0:t1], terms[1][:, t0:t1], ALU.add)
+        for t0, t1 in pieces(UPRIGHT_BLOCKS):
+            nc.vector.tensor_tensor(total[:, t0:t1], two_terms[:, t0:t1], terms[2][:, t0:t1], ALU.add)
+            nc.sync.dma_start(out=out[:, t0:t1], in_=total[:, t0:t1])

@@ -28,6 +28,7 @@ LAST = PASSES - 1
 QUADRANT = 32
 LIVE = 4
 SHARED = 4
+STAGED_STEP = QUADRANT // LIVE
 LIST_COL = 16
 WINDOW = 1024
 MOVED_ROWS = 112
@@ -88,14 +89,13 @@ def tile_moe_ecr_lin_relu2_kernel(tc, xT, w_words, w_scales, b, gate, offs, pos1
             nc.sync.dma_start(out=raw[a][:], in_=xT[a * K_PASS:(a + 1) * K_PASS, :].rearrange("(p j) t -> p j t", j=PACK))
             if a == 0:
                 nc.sync.dma_start(slot_tokens[:], offs)
-            if a == LAST - 1:
-                nc.sync.dma_start(out=bias[:], in_=b)
-                for tile, src in zip(token_slots, (pos1, pos2, pos3)):
-                    nc.sync.dma_start(tile[:], src)
-                nc.sync.dma_start(out=gate_rows[0:CHOICES, :], in_=gate[:, 0, UPRIGHT:T])
 
-        nc.sync.dma_start(out=weight_scales[0:PACK * LIVE, :].bitcast(I32).rearrange("q (g n) -> q g n", g=E * PASSES),
+        nc.sync.dma_start(out=weight_scales[0:P:STAGED_STEP, :].bitcast(I32).rearrange("q (g n) -> q g n", g=E * PASSES),
                           in_=w_scales.bitcast(I32).rearrange("e a q n -> q (e a) n"))
+        nc.sync.dma_start(out=bias[:], in_=b)
+        for tile, src in zip(token_slots, (pos1, pos2, pos3)):
+            nc.sync.dma_start(tile[:], src)
+        nc.sync.dma_start(out=gate_rows[0:CHOICES, :], in_=gate[:, 0, UPRIGHT:T])
 
         def load_weights(dst, e0, e1):
             nc.sync.dma_start(out=dst.bitcast(I32).rearrange("p (g c) -> p g c", g=(e1 - e0) * PASSES),
@@ -103,9 +103,9 @@ def tile_moe_ecr_lin_relu2_kernel(tc, xT, w_words, w_scales, b, gate, offs, pos1
 
         early_weights = keep.tile([P, EARLY * EXPERT_BYTES], U8, name="early_weights", align_bytes=64)
         load_weights(early_weights[:], 0, EARLY)
-        for quad in range(1, P // QUADRANT):
-            nc.sync.dma_start(out=weight_scales[QUADRANT * quad:QUADRANT * quad + LIVE, :].bitcast(I32),
-                              in_=weight_scales[LIVE * quad:LIVE * (quad + 1), :].bitcast(I32))
+        for row in range(1, LIVE):
+            nc.sync.dma_start(out=weight_scales[row:P:QUADRANT, :].bitcast(I32),
+                              in_=weight_scales[STAGED_STEP * row:P:QUADRANT, :].bitcast(I32))
 
         def quantise(a, plane):
             grouped = keep.tile([P, T, PACK], BF16, name=f"grouped{a}", align_bytes=64)

@@ -41,7 +41,7 @@ UPRIGHT = sum(UPRIGHT_BLOCKS)
 TURNED = T - UPRIGHT
 TURNED_BLOCKS = TURNED // P
 
-VECTOR_TOKENS = [448, 288, 160, 160, 0]
+VECTOR_TOKENS = [448, 288, 192, 192, 96]
 LAST_PIECES = [384, 256, 128]
 
 
@@ -178,24 +178,23 @@ def tile_moe_ecr_lin_relu2_kernel(tc, xT, w_words, w_scales, b, gate, offs, pos1
         for s0, s1 in pieces(LAST_PIECES):
             nc.vector.tensor_tensor(y[:, s0:s1], clipped[:, s0:s1], clipped[:, s0:s1], ALU.mult)
 
-        gate_turned = psum.tile([P, TURNED_BLOCKS, P], F32, name="gate_turned", tag=f"bank{E - 1}")
-        for j in range(TURNED_BLOCKS):
-            nc.tensor.transpose(gate_turned[:, j, :], gate_rows[:, j * P:(j + 1) * P], identity[:])
-        gate_columns = keep.tile([P, TURNED_BLOCKS, CHOICES], F32, name="gate_columns")
-        nc.scalar.copy(gate_columns[:], gate_turned[:, :, 0:CHOICES])
-
         def results(r, t0, t1):
             return y[:].indirect(token_slots[r][:, t0 // LIST_COL:t1 // LIST_COL])
 
         blocks = pieces([P] * TURNED_BLOCKS)
         summed = [psum.tile([P, P], F32, name=f"summed{j}", tag=f"bank{CHOICES + j}") for j in range(TURNED_BLOCKS)]
+        gate_columns = keep.tile([P, TURNED_BLOCKS, CHOICES], F32, name="gate_columns")
         gated = keep.tile([P, CHOICES, TURNED], F32, name="gated")
         for r in range(CHOICES):
             fetched = keep.tile([P, TURNED], F32, name=f"fetched{r}")
             nc.scalar.activation(out=fetched[:], in_=results(r, UPRIGHT, T), func=ACT.Copy)
-            turned = psum.tile([P, TURNED], F32, name=f"turned{r}", tag=f"bank{r}")
+            turned = psum.tile([P, 2 * TURNED], F32, name=f"turned{r}", tag=f"bank{r}")
             for t0, t1 in blocks:
                 nc.tensor.transpose(turned[:, t0:t1], fetched[:, t0:t1], identity[:])
+            if r == 0:
+                for t0, t1 in blocks:
+                    nc.tensor.transpose(turned[:, TURNED + t0:TURNED + t1], gate_rows[:, t0:t1], identity[:])
+                nc.scalar.copy(gate_columns[:], turned[:, TURNED:].rearrange("p (j c) -> p j c", c=P)[:, :, 0:CHOICES])
             for j, (t0, t1) in enumerate(blocks):
                 nc.scalar.activation(out=gated[:, r, t0:t1], in_=turned[:, t0:t1], func=ACT.Copy,
                                      scale=gate_columns[:, j, r:r + 1])

@@ -41,7 +41,8 @@ UPRIGHT = sum(UPRIGHT_BLOCKS)
 TURNED = T - UPRIGHT
 TURNED_BLOCKS = TURNED // P
 
-VECTOR_TOKENS = [448, 288, 192, 192, 96]
+VECTOR_TOKENS = [448, 0, 0, 0, 0]
+GPSIMD_TOKENS = [0, 320, 320, 320, 192]
 LAST_PIECES = [384, 256, 128]
 
 
@@ -109,9 +110,11 @@ def tile_moe_ecr_lin_relu2_kernel(tc, xT, w_words, w_scales, b, gate, offs, pos1
 
         def quantise(a, plane):
             grouped = keep.tile([P, T, PACK], BF16, name=f"grouped{a}", align_bytes=64)
-            border = T - VECTOR_TOKENS[a]
+            front, border = GPSIMD_TOKENS[a], T - VECTOR_TOKENS[a]
+            if front:
+                nc.gpsimd.tensor_copy(out=grouped[:, 0:front, :], in_=raw[a][:, :, 0:front].rearrange("p j t -> p t j"))
             for t0, t1 in pieces([CHUNK] * (T // CHUNK)):
-                for c0, c1, on_scalar in ((t0, min(t1, border), True), (max(t0, border), t1, False)):
+                for c0, c1, on_scalar in ((max(t0, front), min(t1, border), True), (max(t0, border), t1, False)):
                     if c0 < c1:
                         dst = grouped[:, c0:c1, :].rearrange("p (c i) j -> p c j i", i=2)
                         src = raw[a][:, :, c0:c1].rearrange("p j (c i) -> p c j i", i=2)

@@ -36,13 +36,13 @@ CHUNK = 256
 PASS_BYTES = 2 * N
 EXPERT_BYTES = PASSES * PASS_BYTES
 EARLY = 3
-UPRIGHT_BLOCKS = [256, 256]
+UPRIGHT_BLOCKS = [384, 128]
 UPRIGHT = sum(UPRIGHT_BLOCKS)
 TURNED = T - UPRIGHT
 TURNED_BLOCKS = TURNED // P
 
 VECTOR_TOKENS = [448, 0, 0, 0, 0]
-GPSIMD_TOKENS = [0, 320, 320, 320, 192]
+GPSIMD_TOKENS = [0, 224, 224, 224, 128]
 LAST_PIECES = [384, 256, 128]
 
 
@@ -113,15 +113,15 @@ def tile_moe_ecr_lin_relu2_kernel(tc, xT, w_words, w_scales, b, gate, offs, pos1
             front, border = GPSIMD_TOKENS[a], T - VECTOR_TOKENS[a]
             if front:
                 nc.gpsimd.tensor_copy(out=grouped[:, 0:front, :], in_=raw[a][:, :, 0:front].rearrange("p j t -> p t j"))
+            cuts = sorted({front, border, T} | {t for t in range(CHUNK, T, CHUNK) if t - front >= CHUNK})
+            for c0, c1 in zip(cuts, cuts[1:]):
+                dst = grouped[:, c0:c1, :].rearrange("p (c i) j -> p c j i", i=2)
+                src = raw[a][:, :, c0:c1].rearrange("p j (c i) -> p c j i", i=2)
+                if c0 < border:
+                    nc.scalar.activation(out=dst, in_=src, func=ACT.Copy)
+                else:
+                    nc.vector.tensor_copy(out=dst, in_=src)
             for t0, t1 in pieces([CHUNK] * (T // CHUNK)):
-                for c0, c1, on_scalar in ((max(t0, front), min(t1, border), True), (max(t0, border), t1, False)):
-                    if c0 < c1:
-                        dst = grouped[:, c0:c1, :].rearrange("p (c i) j -> p c j i", i=2)
-                        src = raw[a][:, :, c0:c1].rearrange("p j (c i) -> p c j i", i=2)
-                        if on_scalar:
-                            nc.scalar.activation(out=dst, in_=src, func=ACT.Copy)
-                        else:
-                            nc.vector.tensor_copy(out=dst, in_=src)
                 nc.vector.quantize_mx(out=token_codes[a][:, t0:t1].bitcast(FP8X4), scales=plane[:, t0:t1],
                                       in_=grouped[:, t0:t1, :].rearrange("p t j -> p (t j)"))
 
@@ -209,12 +209,18 @@ def tile_moe_ecr_lin_relu2_kernel(tc, xT, w_words, w_scales, b, gate, offs, pos1
         nc.scalar.dma_start(out=out[:, UPRIGHT:T], in_=turned_total[:])
 
         terms = [keep.tile([P, UPRIGHT], F32, name=f"term{r}") for r in range(CHOICES)]
-        for r in range(CHOICES):
-            nc.vector.tensor_tensor(terms[r][:], results(r, 0, UPRIGHT), gates[:, r, :], ALU.mult)
         two_terms = keep.tile([P, UPRIGHT], F32, name="two_terms")
         total = keep.tile([P, UPRIGHT], F32, name="total")
-        for t0, t1 in pieces(UPRIGHT_BLOCKS):
-            nc.vector.tensor_tensor(two_terms[:, t0:t1], terms[0][:, t0:t1], terms[1][:, t0:t1], ALU.add)
-        for t0, t1 in pieces(UPRIGHT_BLOCKS):
+
+        def gated_term(r, t0, t1):
+            nc.vector.tensor_tensor(terms[r][:, t0:t1], results(r, t0, t1), gates[:, r, t0:t1], ALU.mult)
+
+        first, second = pieces(UPRIGHT_BLOCKS)
+        gated_term(0, 0, UPRIGHT)
+        gated_term(1, 0, UPRIGHT)
+        gated_term(2, *first)
+        nc.vector.tensor_tensor(two_terms[:], terms[0][:], terms[1][:], ALU.add)
+        gated_term(2, *second)
+        for t0, t1 in (first, second):
             nc.vector.tensor_tensor(total[:, t0:t1], two_terms[:, t0:t1], terms[2][:, t0:t1], ALU.add)
             nc.sync.dma_start(out=out[:, t0:t1], in_=total[:, t0:t1])

@@ -32,6 +32,7 @@ STAGED_STEP = QUADRANT // LIVE
 LIST_COL = 16
 WINDOW = 1024
 MOVED_ROWS = 112
+BURST = 256
 CHUNK = 256
 PASS_BYTES = 2 * N
 EXPERT_BYTES = PASSES * PASS_BYTES
@@ -65,11 +66,11 @@ def tile_moe_ecr_lin_relu2_kernel(tc, xT, w_words, w_scales, b, gate, offs, pos1
         slot_tokens = lists.tile([P, SLOTS // LIST_COL], U16, name="slot_tokens")
         token_slots = [lists.tile([P, T // LIST_COL], U16, name=f"token_slots{r}") for r in range(CHOICES)]
 
-        shared_planes = keep.tile([P, WINDOW], U8, name="shared_planes", tag="planes_then_weights", align_bytes=64)
+        shared_planes = keep.tile([P, WINDOW], U8, name="shared_planes", tag="planes_then_weights", align_bytes=BURST)
         last_plane = keep.tile([P, T], U8, name="last_plane", align_bytes=64)
-        token_codes = [keep.tile([P, WINDOW], U32, name=f"token_codes{a}", tag=f"codes{a}", align_bytes=64) for a in range(PASSES)]
-        moved_planes = [keep.tile([P, SLOTS], U8, name=f"moved_plane{a}", align_bytes=64) for a in range(1, SHARED)]
-        weight_scales = keep.tile([P, E * PASSES * N], U8, name="weight_scales", align_bytes=64)
+        token_codes = [keep.tile([P, WINDOW], U32, name=f"token_codes{a}", tag=f"codes{a}", align_bytes=BURST) for a in range(PASSES)]
+        moved_planes = [keep.tile([P, SLOTS], U8, name=f"moved_plane{a}", align_bytes=BURST) for a in range(1, SHARED)]
+        weight_scales = keep.tile([P, E * PASSES * N], U8, name="weight_scales", align_bytes=BURST)
         y = keep.tile([P, SLOTS + PAD], F32, name="y")
         gate_rows = keep.tile([P, TURNED], F32, name="gate_rows")
         nc.vector.memset(weight_scales[:].bitcast(I32), 0)
@@ -85,7 +86,7 @@ def tile_moe_ecr_lin_relu2_kernel(tc, xT, w_words, w_scales, b, gate, offs, pos1
         make_identity(nc, identity[:])
 
         bias = keep.tile([P, E], F32, name="bias")
-        raw = [keep.tile([P, PACK, T], F32, name=f"raw{a}") for a in range(PASSES)]
+        raw = [keep.tile([P, PACK, T], F32, name=f"raw{a}", align_bytes=BURST) for a in range(PASSES)]
         for a in range(PASSES):
             nc.sync.dma_start(out=raw[a][:], in_=xT[a * K_PASS:(a + 1) * K_PASS, :].rearrange("(p j) t -> p j t", j=PACK))
             if a == 0:
@@ -102,7 +103,7 @@ def tile_moe_ecr_lin_relu2_kernel(tc, xT, w_words, w_scales, b, gate, offs, pos1
             nc.sync.dma_start(out=dst.bitcast(I32).rearrange("p (g c) -> p g c", g=(e1 - e0) * PASSES),
                               in_=w_words.bitcast(I32)[e0:e1].rearrange("e a p c -> p (e a) c"))
 
-        early_weights = keep.tile([P, EARLY * EXPERT_BYTES], U8, name="early_weights", align_bytes=64)
+        early_weights = keep.tile([P, EARLY * EXPERT_BYTES], U8, name="early_weights", align_bytes=BURST)
         load_weights(early_weights[:], 0, EARLY)
         for row in range(1, LIVE):
             nc.sync.dma_start(out=weight_scales[row:P:QUADRANT, :].bitcast(I32),
@@ -126,7 +127,7 @@ def tile_moe_ecr_lin_relu2_kernel(tc, xT, w_words, w_scales, b, gate, offs, pos1
                                       in_=grouped[:, t0:t1, :].rearrange("p t j -> p (t j)"))
 
         slot_codes = [keep.tile([P, SLOTS], U32, name=f"slot_codes{a}", align_bytes=64) for a in range(PASSES)]
-        slot_planes = keep.tile([P, SLOTS], U8, name="slot_planes", align_bytes=64)
+        slot_planes = keep.tile([P, SLOTS], U8, name="slot_planes", align_bytes=BURST)
 
         def gather_codes(a):
             nc.vector.tensor_copy(slot_codes[a][:], token_codes[a][:].indirect(slot_tokens[:]))
@@ -137,14 +138,14 @@ def tile_moe_ecr_lin_relu2_kernel(tc, xT, w_words, w_scales, b, gate, offs, pos1
                 gather_codes(a)
 
         nc.vector.tensor_copy(slot_planes[:], shared_planes[:].indirect(slot_tokens[:]))
-        late_weights = keep.tile([P, (E - EARLY) * EXPERT_BYTES], U8, name="late_weights", tag="planes_then_weights", align_bytes=64)
+        late_weights = keep.tile([P, (E - EARLY) * EXPERT_BYTES], U8, name="late_weights", tag="planes_then_weights", align_bytes=BURST)
         for a in range(1, SHARED):
             nc.sync.dma_start(out=moved_planes[a - 1][0:MOVED_ROWS, :].bitcast(I32),
                               in_=slot_planes[LIVE * a:LIVE * a + MOVED_ROWS, :].bitcast(I32))
             load_weights(late_weights[:, (a - 1) * EXPERT_BYTES:a * EXPERT_BYTES], EARLY + a - 1, EARLY + a)
         gather_codes(SHARED - 1)
 
-        gates = keep.tile([P, CHOICES, UPRIGHT], F32, name="gates", tag=f"codes{SHARED - 1}", align_bytes=64)
+        gates = keep.tile([P, CHOICES, UPRIGHT], F32, name="gates", tag=f"codes{SHARED - 1}", align_bytes=BURST)
         for r in range(CHOICES):
             nc.sync.dma_start(out=gates[:, r, :], in_=gate[r, :, 0:UPRIGHT])
 

@@ -36,7 +36,9 @@ BURST = 256
 CHUNK = 256
 PASS_BYTES = 2 * N
 EXPERT_BYTES = PASSES * PASS_BYTES
-EARLY = 3
+BESIDE = 2
+EARLY = 4
+LATE_LOADS = [[], [PASSES], [PASSES - 2, 2]]
 UPRIGHT_BLOCKS = [384, 128]
 UPRIGHT = sum(UPRIGHT_BLOCKS)
 TURNED = T - UPRIGHT
@@ -63,8 +65,8 @@ def tile_moe_ecr_lin_relu2_kernel(tc, xT, w_words, w_scales, b, gate, offs, pos1
         keep = ctx.enter_context(tc.tile_pool(name="keep", bufs=1))
         psum = ctx.enter_context(tc.psum_pool(name="psum", bufs=1))
 
-        slot_tokens = lists.tile([P, SLOTS // LIST_COL], U16, name="slot_tokens")
-        token_slots = [lists.tile([P, T // LIST_COL], U16, name=f"token_slots{r}") for r in range(CHOICES)]
+        slot_tokens = lists.tile([P, SLOTS // LIST_COL], U16, name="slot_tokens", align_bytes=BURST)
+        token_slots = [lists.tile([P, T // LIST_COL], U16, name=f"token_slots{r}", align_bytes=BURST) for r in range(CHOICES)]
 
         shared_planes = keep.tile([P, WINDOW], U8, name="shared_planes", tag="planes_then_weights", align_bytes=BURST)
         last_plane = keep.tile([P, T], U8, name="last_plane", align_bytes=64)
@@ -86,7 +88,7 @@ def tile_moe_ecr_lin_relu2_kernel(tc, xT, w_words, w_scales, b, gate, offs, pos1
         make_identity(nc, identity[:])
 
         bias = keep.tile([P, E], F32, name="bias")
-        raw = [keep.tile([P, PACK, T], F32, name=f"raw{a}", align_bytes=BURST) for a in range(PASSES)]
+        raw = [keep.tile([P, PACK, T], F32, name=f"raw{a}", tag=f"raw{a}", align_bytes=BURST) for a in range(PASSES)]
         for a in range(PASSES):
             nc.sync.dma_start(out=raw[a][:], in_=xT[a * K_PASS:(a + 1) * K_PASS, :].rearrange("(p j) t -> p j t", j=PACK))
             if a == 0:
@@ -99,12 +101,12 @@ def tile_moe_ecr_lin_relu2_kernel(tc, xT, w_words, w_scales, b, gate, offs, pos1
             nc.sync.dma_start(tile[:], src)
         nc.sync.dma_start(out=gate_rows[0:CHOICES, :], in_=gate[:, 0, UPRIGHT:T])
 
-        def load_weights(dst, e0, e1):
-            nc.sync.dma_start(out=dst.bitcast(I32).rearrange("p (g c) -> p g c", g=(e1 - e0) * PASSES),
-                              in_=w_words.bitcast(I32)[e0:e1].rearrange("e a p c -> p (e a) c"))
+        def load_weights(queue, dst, g0, g1):
+            queue.dma_start(out=dst.bitcast(I32).rearrange("p (g c) -> p g c", g=g1 - g0),
+                            in_=w_words.bitcast(I32).rearrange("e a p c -> p (e a) c")[:, g0:g1, :])
 
-        early_weights = keep.tile([P, EARLY * EXPERT_BYTES], U8, name="early_weights", align_bytes=BURST)
-        load_weights(early_weights[:], 0, EARLY)
+        early_weights = keep.tile([P, (EARLY - BESIDE) * EXPERT_BYTES], U8, name="early_weights", align_bytes=BURST)
+        load_weights(nc.sync, early_weights[:], BESIDE * PASSES, EARLY * PASSES)
         for row in range(1, LIVE):
             nc.sync.dma_start(out=weight_scales[row:P:QUADRANT, :].bitcast(I32),
                               in_=weight_scales[STAGED_STEP * row:P:QUADRANT, :].bitcast(I32))
@@ -137,12 +139,19 @@ def tile_moe_ecr_lin_relu2_kernel(tc, xT, w_words, w_scales, b, gate, offs, pos1
             if a < SHARED - 1:
                 gather_codes(a)
 
+        first_weights = keep.tile([P, BESIDE * EXPERT_BYTES], U8, name="first_weights", tag=f"raw{SHARED - 2}", align_bytes=BURST)
+        load_weights(nc.scalar, first_weights[:], 0, BESIDE * PASSES)
+
         nc.vector.tensor_copy(slot_planes[:], shared_planes[:].indirect(slot_tokens[:]))
         late_weights = keep.tile([P, (E - EARLY) * EXPERT_BYTES], U8, name="late_weights", tag="planes_then_weights", align_bytes=BURST)
+        loaded = 0
         for a in range(1, SHARED):
             nc.sync.dma_start(out=moved_planes[a - 1][0:MOVED_ROWS, :].bitcast(I32),
                               in_=slot_planes[LIVE * a:LIVE * a + MOVED_ROWS, :].bitcast(I32))
-            load_weights(late_weights[:, (a - 1) * EXPERT_BYTES:a * EXPERT_BYTES], EARLY + a - 1, EARLY + a)
+            for count in LATE_LOADS[a - 1]:
+                load_weights(nc.sync, late_weights[:, loaded * PASS_BYTES:(loaded + count) * PASS_BYTES],
+                             EARLY * PASSES + loaded, EARLY * PASSES + loaded + count)
+                loaded = loaded + count
         gather_codes(SHARED - 1)
 
         gates = keep.tile([P, CHOICES, UPRIGHT], F32, name="gates", tag=f"codes{SHARED - 1}", align_bytes=BURST)
@@ -153,7 +162,8 @@ def tile_moe_ecr_lin_relu2_kernel(tc, xT, w_words, w_scales, b, gate, offs, pos1
 
         def multiply(a, e, scales):
             g = e * PASSES + a
-            weights, at = (early_weights, g * PASS_BYTES) if e < EARLY else (late_weights, (g - EARLY * PASSES) * PASS_BYTES)
+            weights, e0 = (first_weights, 0) if e < BESIDE else (early_weights, BESIDE) if e < EARLY else (late_weights, EARLY)
+            at = (g - e0 * PASSES) * PASS_BYTES
             nc.tensor.matmul_mx(
                 out=sums[e][:],
                 lhsT=weights[:, at:at + PASS_BYTES].bitcast(FP4X4),

@@ -34,18 +34,17 @@ WINDOW = 1024
 MOVED_ROWS = 112
 BURST = 256
 CHUNK = 256
-PASS_BYTES = 2 * N
-EXPERT_BYTES = PASSES * PASS_BYTES
-BESIDE = 2
-EARLY = 4
-LATE_LOADS = [[], [PASSES], [PASSES - 2, 2]]
+EXPERT_BYTES = 2 * N
+PASS_BYTES = E * EXPERT_BYTES
+EARLY = 3
 UPRIGHT_BLOCKS = [384, 128]
 UPRIGHT = sum(UPRIGHT_BLOCKS)
 TURNED = T - UPRIGHT
 TURNED_BLOCKS = TURNED // P
+COLUMN_PITCH = 8
 
-VECTOR_TOKENS = [448, 0, 0, 0, 0]
-GPSIMD_TOKENS = [0, 224, 224, 224, 128]
+GPSIMD_TOKENS = [0, 56, 96, 108, 256]
+VECTOR_TOKENS = [400, 280, 220, 200, 0]
 LAST_PIECES = [384, 256, 128]
 
 
@@ -74,9 +73,7 @@ def tile_moe_ecr_lin_relu2_kernel(tc, xT, w_words, w_scales, b, gate, offs, pos1
         moved_planes = [keep.tile([P, SLOTS], U8, name=f"moved_plane{a}", align_bytes=BURST) for a in range(1, SHARED)]
         weight_scales = keep.tile([P, E * PASSES * N], U8, name="weight_scales", align_bytes=BURST)
         y = keep.tile([P, SLOTS + PAD], F32, name="y")
-        gate_rows = keep.tile([P, TURNED], F32, name="gate_rows")
         nc.vector.memset(weight_scales[:].bitcast(I32), 0)
-        nc.vector.memset(gate_rows[:], 0.0)
         nc.vector.memset(shared_planes[:].bitcast(I32), 0)
         for a in range(PASSES):
             nc.vector.memset(token_codes[a][:, T:], 0)
@@ -87,44 +84,42 @@ def tile_moe_ecr_lin_relu2_kernel(tc, xT, w_words, w_scales, b, gate, offs, pos1
         identity = keep.tile([P, P], F32, name="identity")
         make_identity(nc, identity[:])
 
-        bias = keep.tile([P, E], F32, name="bias")
         raw = [keep.tile([P, PACK, T], F32, name=f"raw{a}", tag=f"raw{a}", align_bytes=BURST) for a in range(PASSES)]
         for a in range(PASSES):
+            if a == LAST:
+                nc.sync.dma_start(out=weight_scales[0:P:STAGED_STEP, :].bitcast(I32).rearrange("q (g n) -> q g n", g=E * PASSES),
+                                  in_=w_scales.bitcast(I32).rearrange("e a q n -> q (e a) n"))
             nc.sync.dma_start(out=raw[a][:], in_=xT[a * K_PASS:(a + 1) * K_PASS, :].rearrange("(p j) t -> p j t", j=PACK))
             if a == 0:
                 nc.sync.dma_start(slot_tokens[:], offs)
-
-        nc.sync.dma_start(out=weight_scales[0:P:STAGED_STEP, :].bitcast(I32).rearrange("q (g n) -> q g n", g=E * PASSES),
-                          in_=w_scales.bitcast(I32).rearrange("e a q n -> q (e a) n"))
-        nc.sync.dma_start(out=bias[:], in_=b)
-        for tile, src in zip(token_slots, (pos1, pos2, pos3)):
-            nc.sync.dma_start(tile[:], src)
-        nc.sync.dma_start(out=gate_rows[0:CHOICES, :], in_=gate[:, 0, UPRIGHT:T])
-
-        def load_weights(queue, dst, g0, g1):
-            queue.dma_start(out=dst.bitcast(I32).rearrange("p (g c) -> p g c", g=g1 - g0),
-                            in_=w_words.bitcast(I32).rearrange("e a p c -> p (e a) c")[:, g0:g1, :])
-
-        early_weights = keep.tile([P, (EARLY - BESIDE) * EXPERT_BYTES], U8, name="early_weights", align_bytes=BURST)
-        load_weights(nc.sync, early_weights[:], BESIDE * PASSES, EARLY * PASSES)
         for row in range(1, LIVE):
             nc.sync.dma_start(out=weight_scales[row:P:QUADRANT, :].bitcast(I32),
                               in_=weight_scales[STAGED_STEP * row:P:QUADRANT, :].bitcast(I32))
 
+        def load_weights(dst, a, e0, e1):
+            nc.sync.dma_start(out=dst[:, e0 * EXPERT_BYTES:e1 * EXPERT_BYTES].bitcast(I32).rearrange("p (e c) -> p e c", e=e1 - e0),
+                              in_=w_words.bitcast(I32).rearrange("e a p c -> a p e c")[a, :, e0:e1, :])
+
+        weights = [keep.tile([P, PASS_BYTES], U8, name=f"weights{a}", align_bytes=BURST)[:] for a in range(EARLY)]
+        for a in range(EARLY):
+            load_weights(weights[a], a, 0, E)
+
         def quantise(a, plane):
             grouped = keep.tile([P, T, PACK], BF16, name=f"grouped{a}", align_bytes=64)
-            front, border = GPSIMD_TOKENS[a], T - VECTOR_TOKENS[a]
+
+            def walk(c0, c1):
+                return dict(out=grouped[:, c0:c1, :].rearrange("p (c i) j -> p c j i", i=2),
+                            in_=raw[a][:, :, c0:c1].rearrange("p j (c i) -> p c j i", i=2))
+
+            front, last = GPSIMD_TOKENS[a], T - CHUNK
+            border = last - VECTOR_TOKENS[a]
             if front:
                 nc.gpsimd.tensor_copy(out=grouped[:, 0:front, :], in_=raw[a][:, :, 0:front].rearrange("p j t -> p t j"))
-            cuts = sorted({front, border, T} | {t for t in range(CHUNK, T, CHUNK) if t - front >= CHUNK})
-            for c0, c1 in zip(cuts, cuts[1:]):
-                dst = grouped[:, c0:c1, :].rearrange("p (c i) j -> p c j i", i=2)
-                src = raw[a][:, :, c0:c1].rearrange("p j (c i) -> p c j i", i=2)
-                if c0 < border:
-                    nc.scalar.activation(out=dst, in_=src, func=ACT.Copy)
-                else:
-                    nc.vector.tensor_copy(out=dst, in_=src)
-            for t0, t1 in pieces([CHUNK] * (T // CHUNK)):
+            nc.scalar.activation(func=ACT.Copy, **walk(front, border))
+            if border < last:
+                nc.vector.tensor_copy(**walk(border, last))
+            nc.scalar.activation(func=ACT.Copy, **walk(last, T))
+            for t0, t1 in pieces([CHUNK, CHUNK, CHUNK] if border < last else [last, CHUNK]):
                 nc.vector.quantize_mx(out=token_codes[a][:, t0:t1].bitcast(FP8X4), scales=plane[:, t0:t1],
                                       in_=grouped[:, t0:t1, :].rearrange("p t j -> p (t j)"))
 
@@ -139,42 +134,52 @@ def tile_moe_ecr_lin_relu2_kernel(tc, xT, w_words, w_scales, b, gate, offs, pos1
             if a < SHARED - 1:
                 gather_codes(a)
 
-        first_weights = keep.tile([P, BESIDE * EXPERT_BYTES], U8, name="first_weights", tag=f"raw{SHARED - 2}", align_bytes=BURST)
-        load_weights(nc.scalar, first_weights[:], 0, BESIDE * PASSES)
-
         nc.vector.tensor_copy(slot_planes[:], shared_planes[:].indirect(slot_tokens[:]))
-        late_weights = keep.tile([P, (E - EARLY) * EXPERT_BYTES], U8, name="late_weights", tag="planes_then_weights", align_bytes=BURST)
-        loaded = 0
-        for a in range(1, SHARED):
+        late_weights = keep.tile([P, (PASSES - EARLY) * PASS_BYTES], U8, name="late_weights", tag="planes_then_weights", align_bytes=BURST)
+
+        def move_plane(a):
             nc.sync.dma_start(out=moved_planes[a - 1][0:MOVED_ROWS, :].bitcast(I32),
                               in_=slot_planes[LIVE * a:LIVE * a + MOVED_ROWS, :].bitcast(I32))
-            for count in LATE_LOADS[a - 1]:
-                load_weights(nc.sync, late_weights[:, loaded * PASS_BYTES:(loaded + count) * PASS_BYTES],
-                             EARLY * PASSES + loaded, EARLY * PASSES + loaded + count)
-                loaded = loaded + count
+
+        weights.extend(late_weights[:, i * PASS_BYTES:(i + 1) * PASS_BYTES] for i in range(PASSES - EARLY))
+        move_plane(1)
+        move_plane(2)
+        load_weights(weights[3], 3, 0, E)
+        move_plane(3)
+        load_weights(weights[LAST], LAST, 0, E // 2)
+        load_weights(weights[LAST], LAST, E // 2, E)
         gather_codes(SHARED - 1)
 
+        bias = keep.tile([P, E], F32, name="bias")
+        nc.sync.dma_start(out=bias[:], in_=b)
+        for tile, src in zip(token_slots, (pos1, pos2, pos3)):
+            nc.sync.dma_start(tile[:], src)
+
         gates = keep.tile([P, CHOICES, UPRIGHT], F32, name="gates", tag=f"codes{SHARED - 1}", align_bytes=BURST)
+        gate_columns = keep.tile([P, TURNED_BLOCKS, COLUMN_PITCH], F32, name="gate_columns")
         for r in range(CHOICES):
             nc.sync.dma_start(out=gates[:, r, :], in_=gate[r, :, 0:UPRIGHT])
+            if r == 0:
+                with nc.allow_non_contiguous_dma(reason="one gate a partition"):
+                    for j in range(TURNED_BLOCKS):
+                        nc.sync.dma_start(out=gate_columns[:, j, 0:CHOICES],
+                                          in_=gate[:, 0, UPRIGHT + j * P:UPRIGHT + (j + 1) * P].rearrange("r p -> p r"))
 
         sums = [psum.tile([P, C], F32, name=f"sums{e}", tag=f"bank{e}") for e in range(E)]
+        pass_planes = [slot_planes] + moved_planes
 
         def multiply(a, e, scales):
             g = e * PASSES + a
-            weights, e0 = (first_weights, 0) if e < BESIDE else (early_weights, BESIDE) if e < EARLY else (late_weights, EARLY)
-            at = (g - e0 * PASSES) * PASS_BYTES
             nc.tensor.matmul_mx(
                 out=sums[e][:],
-                lhsT=weights[:, at:at + PASS_BYTES].bitcast(FP4X4),
+                lhsT=weights[a][:, e * EXPERT_BYTES:(e + 1) * EXPERT_BYTES].bitcast(FP4X4),
                 lhsT_scale=weight_scales[:, g * N:(g + 1) * N],
                 rhs=slot_codes[a][:, e * C:(e + 1) * C].bitcast(FP8X4),
                 rhs_scale=scales,
                 start=(a == 0), stop=(a == LAST))
 
-        pass_planes = [slot_planes] + moved_planes
         for a in range(SHARED):
-            for e in range(EARLY):
+            for e in range(E):
                 multiply(a, e, pass_planes[a][:, e * C:(e + 1) * C])
 
         quantise(LAST, last_plane[:])
@@ -184,9 +189,6 @@ def tile_moe_ecr_lin_relu2_kernel(tc, xT, w_words, w_scales, b, gate, offs, pos1
             last_scales = keep.tile([P, s1 - s0], U8, name=f"slot_scales{s0}", align_bytes=64)
             nc.vector.tensor_copy(last_scales[:], last_plane[:].indirect(slot_tokens[:, s0 // LIST_COL:s1 // LIST_COL]))
             for e in range(s0 // C, s1 // C):
-                if e >= EARLY:
-                    for a in range(SHARED):
-                        multiply(a, e, pass_planes[a][:, e * C:(e + 1) * C])
                 multiply(LAST, e, last_scales[:, e * C - s0:(e + 1) * C - s0])
                 nc.scalar.activation(out=clipped[:, e * C:(e + 1) * C], in_=sums[e][:], func=ACT.Relu, bias=bias[:, e:e + 1])
         for s0, s1 in pieces(LAST_PIECES):
@@ -197,27 +199,22 @@ def tile_moe_ecr_lin_relu2_kernel(tc, xT, w_words, w_scales, b, gate, offs, pos1
 
         blocks = pieces([P] * TURNED_BLOCKS)
         summed = [psum.tile([P, P], F32, name=f"summed{j}", tag=f"bank{CHOICES + j}") for j in range(TURNED_BLOCKS)]
-        gate_columns = keep.tile([P, TURNED_BLOCKS, CHOICES], F32, name="gate_columns")
         gated = keep.tile([P, CHOICES, TURNED], F32, name="gated")
+        turned = [psum.tile([P, TURNED], F32, name=f"turned{r}", tag=f"bank{r}") for r in range(CHOICES)]
         for r in range(CHOICES):
             fetched = keep.tile([P, TURNED], F32, name=f"fetched{r}")
             nc.scalar.activation(out=fetched[:], in_=results(r, UPRIGHT, T), func=ACT.Copy)
-            turned = psum.tile([P, 2 * TURNED], F32, name=f"turned{r}", tag=f"bank{r}")
             for t0, t1 in blocks:
-                nc.tensor.transpose(turned[:, t0:t1], fetched[:, t0:t1], identity[:])
-            if r == 0:
-                for t0, t1 in blocks:
-                    nc.tensor.transpose(turned[:, TURNED + t0:TURNED + t1], gate_rows[:, t0:t1], identity[:])
-                nc.scalar.copy(gate_columns[:], turned[:, TURNED:].rearrange("p (j c) -> p j c", c=P)[:, :, 0:CHOICES])
+                nc.tensor.transpose(turned[r][:, t0:t1], fetched[:, t0:t1], identity[:])
             for j, (t0, t1) in enumerate(blocks):
-                nc.scalar.activation(out=gated[:, r, t0:t1], in_=turned[:, t0:t1], func=ACT.Copy,
+                nc.scalar.activation(out=gated[:, r, t0:t1], in_=turned[r][:, t0:t1], func=ACT.Copy,
                                      scale=gate_columns[:, j, r:r + 1])
                 nc.tensor.matmul(summed[j][:], gated[:, r, t0:t1], identity[:], is_transpose=True,
                                  start=(r == 0), stop=(r == CHOICES - 1))
         turned_total = keep.tile([P, TURNED], F32, name="turned_total")
         for j, (t0, t1) in enumerate(blocks):
             nc.scalar.copy(turned_total[:, t0:t1], summed[j][:])
-        nc.scalar.dma_start(out=out[:, UPRIGHT:T], in_=turned_total[:])
+            nc.scalar.dma_start(out=out[:, UPRIGHT + t0:UPRIGHT + t1], in_=turned_total[:, t0:t1])
 
         terms = [keep.tile([P, UPRIGHT], F32, name=f"term{r}") for r in range(CHOICES)]
         two_terms = keep.tile([P, UPRIGHT], F32, name="two_terms")

@@ -36,15 +36,15 @@ BURST = 256
 CHUNK = 256
 EXPERT_BYTES = 2 * N
 PASS_BYTES = E * EXPERT_BYTES
-EARLY = 3
+EARLY = 2
 UPRIGHT_BLOCKS = [384, 128]
 UPRIGHT = sum(UPRIGHT_BLOCKS)
 TURNED = T - UPRIGHT
 TURNED_BLOCKS = TURNED // P
 COLUMN_PITCH = 8
 
-GPSIMD_TOKENS = [0, 56, 96, 108, 256]
-VECTOR_TOKENS = [400, 280, 220, 200, 0]
+GPSIMD_TOKENS = [0, 224, 224, 224, 192]
+VECTOR_TOKENS = [400, 0, 0, 0, 0]
 LAST_PIECES = [384, 256, 128]
 
 
@@ -104,6 +104,11 @@ def tile_moe_ecr_lin_relu2_kernel(tc, xT, w_words, w_scales, b, gate, offs, pos1
         for a in range(EARLY):
             load_weights(weights[a], a, 0, E)
 
+        bias = keep.tile([P, E], F32, name="bias")
+        nc.sync.dma_start(out=bias[:], in_=b)
+        for tile, src in zip(token_slots, (pos1, pos2, pos3)):
+            nc.sync.dma_start(tile[:], src)
+
         def quantise(a, plane):
             grouped = keep.tile([P, T, PACK], BF16, name=f"grouped{a}", align_bytes=64)
 
@@ -142,18 +147,13 @@ def tile_moe_ecr_lin_relu2_kernel(tc, xT, w_words, w_scales, b, gate, offs, pos1
                               in_=slot_planes[LIVE * a:LIVE * a + MOVED_ROWS, :].bitcast(I32))
 
         weights.extend(late_weights[:, i * PASS_BYTES:(i + 1) * PASS_BYTES] for i in range(PASSES - EARLY))
-        move_plane(1)
-        move_plane(2)
-        load_weights(weights[3], 3, 0, E)
-        move_plane(3)
+        for a in range(1, SHARED):
+            if a >= EARLY:
+                load_weights(weights[a], a, 0, E)
+            move_plane(a)
         load_weights(weights[LAST], LAST, 0, E // 2)
         load_weights(weights[LAST], LAST, E // 2, E)
         gather_codes(SHARED - 1)
-
-        bias = keep.tile([P, E], F32, name="bias")
-        nc.sync.dma_start(out=bias[:], in_=b)
-        for tile, src in zip(token_slots, (pos1, pos2, pos3)):
-            nc.sync.dma_start(tile[:], src)
 
         gates = keep.tile([P, CHOICES, UPRIGHT], F32, name="gates", tag=f"codes{SHARED - 1}", align_bytes=BURST)
         gate_columns = keep.tile([P, TURNED_BLOCKS, COLUMN_PITCH], F32, name="gate_columns")

@@ -33,6 +33,7 @@ LIST_COL = 16
 WINDOW = 1024
 MOVED_ROWS = 112
 BURST = 256
+RUN = 4
 CHUNK = 256
 EXPERT_BYTES = 2 * N
 PASS_BYTES = E * EXPERT_BYTES
@@ -113,8 +114,8 @@ def tile_moe_ecr_lin_relu2_kernel(tc, xT, w_words, w_scales, b, gate, offs, pos1
             grouped = keep.tile([P, T, PACK], BF16, name=f"grouped{a}", align_bytes=64)
 
             def walk(c0, c1):
-                return dict(out=grouped[:, c0:c1, :].rearrange("p (c i) j -> p c j i", i=2),
-                            in_=raw[a][:, :, c0:c1].rearrange("p j (c i) -> p c j i", i=2))
+                return dict(out=grouped[:, c0:c1, :].rearrange("p (c i) j -> p c j i", i=RUN),
+                            in_=raw[a][:, :, c0:c1].rearrange("p j (c i) -> p c j i", i=RUN))
 
             front, last = GPSIMD_TOKENS[a], T - CHUNK
             border = last - VECTOR_TOKENS[a]
@@ -123,8 +124,10 @@ def tile_moe_ecr_lin_relu2_kernel(tc, xT, w_words, w_scales, b, gate, offs, pos1
             nc.scalar.activation(func=ACT.Copy, **walk(front, border))
             if border < last:
                 nc.vector.tensor_copy(**walk(border, last))
-            nc.scalar.activation(func=ACT.Copy, **walk(last, T))
-            for t0, t1 in pieces([CHUNK, CHUNK, CHUNK] if border < last else [last, CHUNK]):
+            ending = [CHUNK] if a == LAST else [CHUNK // 2, CHUNK // 2]
+            for c0, c1 in pieces([last] + ending)[1:]:
+                nc.scalar.activation(func=ACT.Copy, **walk(c0, c1))
+            for t0, t1 in pieces(([CHUNK, CHUNK] if border < last else [last]) + ending):
                 nc.vector.quantize_mx(out=token_codes[a][:, t0:t1].bitcast(FP8X4), scales=plane[:, t0:t1],
                                       in_=grouped[:, t0:t1, :].rearrange("p t j -> p (t j)"))
 

@@ -34,6 +34,7 @@ WINDOW = 1024
 MOVED_ROWS = 112
 BURST = 256
 RUN = 4
+HELD = 128
 CHUNK = 256
 EXPERT_BYTES = 2 * N
 PASS_BYTES = E * EXPERT_BYTES
@@ -46,7 +47,7 @@ COLUMN_PITCH = 8
 
 GPSIMD_TOKENS = [0, 224, 224, 224, 192]
 VECTOR_TOKENS = [400, 0, 0, 0, 0]
-LAST_PIECES = [384, 256, 128]
+LAST_PIECES = [256, 256, 128, 128]
 
 
 def pieces(widths):
@@ -156,8 +157,34 @@ def tile_moe_ecr_lin_relu2_kernel(tc, xT, w_words, w_scales, b, gate, offs, pos1
             move_plane(a)
         load_weights(weights[LAST], LAST, 0, E // 2)
         load_weights(weights[LAST], LAST, E // 2, E)
-        gather_codes(SHARED - 1)
+        nc.vector.tensor_copy(slot_codes[SHARED - 1][:, 0:SLOTS - HELD],
+                              token_codes[SHARED - 1][:].indirect(slot_tokens[:, 0:(SLOTS - HELD) // LIST_COL]))
 
+        sums = [psum.tile([P, C], F32, name=f"sums{e}", tag=f"bank{e}") for e in range(E)]
+        pass_planes = [slot_planes] + moved_planes
+
+        codes = {}
+
+        def multiply(a, e, scales):
+            g = e * PASSES + a
+            nc.tensor.matmul_mx(
+                out=sums[e][:],
+                lhsT=weights[a][:, e * EXPERT_BYTES:(e + 1) * EXPERT_BYTES].bitcast(FP4X4),
+                lhsT_scale=weight_scales[:, g * N:(g + 1) * N],
+                rhs=codes.get((a, e), slot_codes[a][:, e * C:(e + 1) * C]).bitcast(FP8X4),
+                rhs_scale=scales,
+                start=(a == 0), stop=(a == LAST))
+
+        for a in range(SHARED):
+            for e in range(E if a < SHARED - 1 else E - HELD // C):
+                multiply(a, e, pass_planes[a][:, e * C:(e + 1) * C])
+
+        quantise(LAST, last_plane[:])
+        held_codes = keep.tile([P, HELD], U32, name="held_codes", tag=f"raw{LAST}", align_bytes=BURST)
+        nc.vector.tensor_copy(held_codes[:], token_codes[SHARED - 1][:].indirect(slot_tokens[:, (SLOTS - HELD) // LIST_COL:]))
+        for e in range(E - HELD // C, E):
+            codes[SHARED - 1, e] = held_codes[:, e * C - (SLOTS - HELD):(e + 1) * C - (SLOTS - HELD)]
+            multiply(SHARED - 1, e, pass_planes[SHARED - 1][:, e * C:(e + 1) * C])
         gates = keep.tile([P, CHOICES, UPRIGHT], F32, name="gates", tag=f"codes{SHARED - 1}", align_bytes=BURST)
         gate_columns = keep.tile([P, TURNED_BLOCKS, COLUMN_PITCH], F32, name="gate_columns")
         for r in range(CHOICES):
@@ -168,24 +195,6 @@ def tile_moe_ecr_lin_relu2_kernel(tc, xT, w_words, w_scales, b, gate, offs, pos1
                         nc.sync.dma_start(out=gate_columns[:, j, 0:CHOICES],
                                           in_=gate[:, 0, UPRIGHT + j * P:UPRIGHT + (j + 1) * P].rearrange("r p -> p r"))
 
-        sums = [psum.tile([P, C], F32, name=f"sums{e}", tag=f"bank{e}") for e in range(E)]
-        pass_planes = [slot_planes] + moved_planes
-
-        def multiply(a, e, scales):
-            g = e * PASSES + a
-            nc.tensor.matmul_mx(
-                out=sums[e][:],
-                lhsT=weights[a][:, e * EXPERT_BYTES:(e + 1) * EXPERT_BYTES].bitcast(FP4X4),
-                lhsT_scale=weight_scales[:, g * N:(g + 1) * N],
-                rhs=slot_codes[a][:, e * C:(e + 1) * C].bitcast(FP8X4),
-                rhs_scale=scales,
-                start=(a == 0), stop=(a == LAST))
-
-        for a in range(SHARED):
-            for e in range(E):
-                multiply(a, e, pass_planes[a][:, e * C:(e + 1) * C])
-
-        quantise(LAST, last_plane[:])
         gather_codes(LAST)
         clipped = keep.tile([P, SLOTS], F32, name="clipped")
         for s0, s1 in pieces(LAST_PIECES):

@@ -35,6 +35,7 @@ MOVED_ROWS = 112
 BURST = 256
 RUN = 4
 HELD = 128
+WARM_UPS = 3
 CHUNK = 256
 EXPERT_BYTES = 2 * N
 PASS_BYTES = E * EXPERT_BYTES
@@ -178,6 +179,16 @@ def tile_moe_ecr_lin_relu2_kernel(tc, xT, w_words, w_scales, b, gate, offs, pos1
         for a in range(SHARED):
             for e in range(E if a < SHARED - 1 else E - HELD // C):
                 multiply(a, e, pass_planes[a][:, e * C:(e + 1) * C])
+            if a == 0:
+                idle = psum.tile([P, WARM_UPS, C], F32, name="idle", tag=f"bank{E}")
+                for e in range(WARM_UPS):
+                    nc.tensor.matmul_mx(
+                        out=idle[:, e, :],
+                        lhsT=weights[0][:, e * EXPERT_BYTES:(e + 1) * EXPERT_BYTES].bitcast(FP4X4),
+                        lhsT_scale=weight_scales[:, e * PASSES * N:(e * PASSES + 1) * N],
+                        rhs=slot_codes[0][:, e * C:(e + 1) * C].bitcast(FP8X4),
+                        rhs_scale=slot_planes[:, e * C:(e + 1) * C],
+                        start=True, stop=True)
 
         quantise(LAST, last_plane[:])
         held_codes = keep.tile([P, HELD], U32, name="held_codes", tag=f"raw{LAST}", align_bytes=BURST)

@@ -33,7 +33,7 @@ LIST_COL = 16
 WINDOW = 1024
 MOVED_ROWS = 112
 BURST = 256
-RUN = 4
+RUN = 2
 HELD = 128
 WARM_UPS = 3
 CHUNK = 256
@@ -46,7 +46,7 @@ TURNED = T - UPRIGHT
 TURNED_BLOCKS = TURNED // P
 COLUMN_PITCH = 8
 
-GPSIMD_TOKENS = [0, 224, 224, 224, 192]
+GPSIMD_TOKENS = [0, 288, 288, 288, 192]
 VECTOR_TOKENS = [400, 0, 0, 0, 0]
 LAST_PIECES = [256, 256, 128, 128]
 
@@ -122,7 +122,7 @@ def tile_moe_ecr_lin_relu2_kernel(tc, xT, w_words, w_scales, b, gate, offs, pos1
             front, last = GPSIMD_TOKENS[a], T - CHUNK
             border = last - VECTOR_TOKENS[a]
             if front:
-                nc.gpsimd.tensor_copy(out=grouped[:, 0:front, :], in_=raw[a][:, :, 0:front].rearrange("p j t -> p t j"))
+                nc.gpsimd.tensor_copy(**walk(0, front))
             nc.scalar.activation(func=ACT.Copy, **walk(front, border))
             if border < last:
                 nc.vector.tensor_copy(**walk(border, last))

@@ -46,7 +46,7 @@ TURNED = T - UPRIGHT
 TURNED_BLOCKS = TURNED // P
 COLUMN_PITCH = 8
 
-GPSIMD_TOKENS = [0, 288, 288, 288, 192]
+GPSIMD_TOKENS = [0, 256, 256, 256, 256]
 VECTOR_TOKENS = [400, 0, 0, 0, 0]
 LAST_PIECES = [256, 256, 128, 128]
 

@@ -34,13 +34,13 @@ WINDOW = 1024
 MOVED_ROWS = 112
 BURST = 256
 RUN = 2
-HELD = 128
+HELD = C
 WARM_UPS = 3
 CHUNK = 256
 EXPERT_BYTES = 2 * N
 PASS_BYTES = E * EXPERT_BYTES
 EARLY = 2
-UPRIGHT_BLOCKS = [384, 128]
+UPRIGHT_BLOCKS = [256, 256]
 UPRIGHT = sum(UPRIGHT_BLOCKS)
 TURNED = T - UPRIGHT
 TURNED_BLOCKS = TURNED // P
@@ -191,11 +191,13 @@ def tile_moe_ecr_lin_relu2_kernel(tc, xT, w_words, w_scales, b, gate, offs, pos1
                         start=True, stop=True)
 
         quantise(LAST, last_plane[:])
+
         held_codes = keep.tile([P, HELD], U32, name="held_codes", tag=f"raw{LAST}", align_bytes=BURST)
         nc.vector.tensor_copy(held_codes[:], token_codes[SHARED - 1][:].indirect(slot_tokens[:, (SLOTS - HELD) // LIST_COL:]))
         for e in range(E - HELD // C, E):
             codes[SHARED - 1, e] = held_codes[:, e * C - (SLOTS - HELD):(e + 1) * C - (SLOTS - HELD)]
             multiply(SHARED - 1, e, pass_planes[SHARED - 1][:, e * C:(e + 1) * C])
+
         gates = keep.tile([P, CHOICES, UPRIGHT], F32, name="gates", tag=f"codes{SHARED - 1}", align_bytes=BURST)
         gate_columns = keep.tile([P, TURNED_BLOCKS, COLUMN_PITCH], F32, name="gate_columns")
         for r in range(CHOICES):

@@ -39,6 +39,7 @@ WARM_UPS = 3
 CHUNK = 256
 EXPERT_BYTES = 2 * N
 PASS_BYTES = E * EXPERT_BYTES
+SPLIT = SHARED - 1
 EARLY = 2
 UPRIGHT_BLOCKS = [256, 256]
 UPRIGHT = sum(UPRIGHT_BLOCKS)
@@ -46,8 +47,7 @@ TURNED = T - UPRIGHT
 TURNED_BLOCKS = TURNED // P
 COLUMN_PITCH = 8
 
-GPSIMD_TOKENS = [0, 256, 256, 256, 256]
-VECTOR_TOKENS = [400, 0, 0, 0, 0]
+VECTOR_TOKENS = 400
 LAST_PIECES = [256, 256, 128, 128]
 
 
@@ -87,12 +87,15 @@ def tile_moe_ecr_lin_relu2_kernel(tc, xT, w_words, w_scales, b, gate, offs, pos1
         identity = keep.tile([P, P], F32, name="identity")
         make_identity(nc, identity[:])
 
-        raw = [keep.tile([P, PACK, T], F32, name=f"raw{a}", tag=f"raw{a}", align_bytes=BURST) for a in range(PASSES)]
+        landings = [pieces([T] if a < SPLIT else [T - CHUNK, CHUNK]) for a in range(PASSES)]
+        raw = [[keep.tile([P, PACK, t1 - t0], F32, name=f"raw{a}_{t0}", tag=f"raw{a}_{t0}", align_bytes=BURST) for t0, t1 in landings[a]]
+               for a in range(PASSES)]
         for a in range(PASSES):
             if a == LAST:
                 nc.sync.dma_start(out=weight_scales[0:P:STAGED_STEP, :].bitcast(I32).rearrange("q (g n) -> q g n", g=E * PASSES),
                                   in_=w_scales.bitcast(I32).rearrange("e a q n -> q (e a) n"))
-            nc.sync.dma_start(out=raw[a][:], in_=xT[a * K_PASS:(a + 1) * K_PASS, :].rearrange("(p j) t -> p j t", j=PACK))
+            for tile, (t0, t1) in zip(raw[a], landings[a]):
+                nc.sync.dma_start(out=tile[:], in_=xT[a * K_PASS:(a + 1) * K_PASS, t0:t1].rearrange("(p j) t -> p j t", j=PACK))
             if a == 0:
                 nc.sync.dma_start(slot_tokens[:], offs)
         for row in range(1, LIVE):
@@ -113,25 +116,32 @@ def tile_moe_ecr_lin_relu2_kernel(tc, xT, w_words, w_scales, b, gate, offs, pos1
             nc.sync.dma_start(tile[:], src)
 
         def quantise(a, plane):
-            grouped = keep.tile([P, T, PACK], BF16, name=f"grouped{a}", align_bytes=64)
+            chunks = pieces([CHUNK] * (T // CHUNK))
+            tags = [f"last_chunk{a - 1}" if a >= SPLIT else f"first_chunk{a}", f"second_chunk{a}", f"last_chunk{a}"]
+            grouped = [keep.tile([P, CHUNK, PACK], BF16, name=f"grouped{a}_{i}", tag=tag, align_bytes=64) for i, tag in enumerate(tags)]
 
             def walk(c0, c1):
-                return dict(out=grouped[:, c0:c1, :].rearrange("p (c i) j -> p c j i", i=RUN),
-                            in_=raw[a][:, :, c0:c1].rearrange("p j (c i) -> p c j i", i=RUN))
+                i = c0 // CHUNK
+                piece = max(n for n, (t0, t1) in enumerate(landings[a]) if t0 <= c0)
+                first = landings[a][piece][0]
+                return dict(out=grouped[i][:, c0 - i * CHUNK:c1 - i * CHUNK, :].rearrange("p (c i) j -> p c j i", i=RUN),
+                            in_=raw[a][piece][:, :, c0 - first:c1 - first].rearrange("p j (c i) -> p c j i", i=RUN))
 
-            front, last = GPSIMD_TOKENS[a], T - CHUNK
-            border = last - VECTOR_TOKENS[a]
-            if front:
-                nc.gpsimd.tensor_copy(**walk(0, front))
-            nc.scalar.activation(func=ACT.Copy, **walk(front, border))
-            if border < last:
-                nc.vector.tensor_copy(**walk(border, last))
+            last = T - CHUNK
+            if a == 0:
+                nc.scalar.activation(func=ACT.Copy, **walk(0, last - VECTOR_TOKENS))
+                nc.vector.tensor_copy(**walk(last - VECTOR_TOKENS, CHUNK))
+                nc.vector.tensor_copy(**walk(CHUNK, last))
+            else:
+                nc.gpsimd.tensor_copy(**walk(*chunks[0]))
+                nc.scalar.activation(func=ACT.Copy, **walk(*chunks[1]))
             ending = [CHUNK] if a == LAST else [CHUNK // 2, CHUNK // 2]
             for c0, c1 in pieces([last] + ending)[1:]:
                 nc.scalar.activation(func=ACT.Copy, **walk(c0, c1))
-            for t0, t1 in pieces(([CHUNK, CHUNK] if border < last else [last]) + ending):
+            for t0, t1 in pieces([CHUNK, CHUNK] + ending):
+                i = t0 // CHUNK
                 nc.vector.quantize_mx(out=token_codes[a][:, t0:t1].bitcast(FP8X4), scales=plane[:, t0:t1],
-                                      in_=grouped[:, t0:t1, :].rearrange("p t j -> p (t j)"))
+                                      in_=grouped[i][:, t0 - i * CHUNK:t1 - i * CHUNK, :].rearrange("p t j -> p (t j)"))
 
         slot_codes = [keep.tile([P, SLOTS], U32, name=f"slot_codes{a}", align_bytes=64) for a in range(PASSES)]
         slot_planes = keep.tile([P, SLOTS], U8, name="slot_planes", align_bytes=BURST)
@@ -192,7 +202,7 @@ def tile_moe_ecr_lin_relu2_kernel(tc, xT, w_words, w_scales, b, gate, offs, pos1
 
         quantise(LAST, last_plane[:])
 
-        held_codes = keep.tile([P, HELD], U32, name="held_codes", tag=f"raw{LAST}", align_bytes=BURST)
+        held_codes = keep.tile([P, HELD], U32, name="held_codes", tag=f"raw{LAST}_{T - CHUNK}", align_bytes=BURST)
         nc.vector.tensor_copy(held_codes[:], token_codes[SHARED - 1][:].indirect(slot_tokens[:, (SLOTS - HELD) // LIST_COL:]))
         for e in range(E - HELD // C, E):
             codes[SHARED - 1, e] = held_codes[:, e * C - (SLOTS - HELD):(e + 1) * C - (SLOTS - HELD)]

@@ -112,8 +112,6 @@ def tile_moe_ecr_lin_relu2_kernel(tc, xT, w_words, w_scales, b, gate, offs, pos1
 
         bias = keep.tile([P, E], F32, name="bias")
         nc.sync.dma_start(out=bias[:], in_=b)
-        for tile, src in zip(token_slots, (pos1, pos2, pos3)):
-            nc.sync.dma_start(tile[:], src)
 
         def quantise(a, plane):
             chunks = pieces([CHUNK] * (T // CHUNK))
@@ -146,13 +144,22 @@ def tile_moe_ecr_lin_relu2_kernel(tc, xT, w_words, w_scales, b, gate, offs, pos1
         slot_codes = [keep.tile([P, SLOTS], U32, name=f"slot_codes{a}", align_bytes=64) for a in range(PASSES)]
         slot_planes = keep.tile([P, SLOTS], U8, name="slot_planes", align_bytes=BURST)
 
-        def gather_codes(a):
-            nc.vector.tensor_copy(slot_codes[a][:], token_codes[a][:].indirect(slot_tokens[:]))
+        codes = {}
+
+        def gather_codes(a, slots=SLOTS):
+            nc.vector.tensor_copy(slot_codes[a][:, 0:slots], token_codes[a][:].indirect(slot_tokens[:, 0:slots // LIST_COL]))
+
+        def gather_held(a):
+            held = keep.tile([P, HELD], U32, name=f"held_codes{a}", tag=f"raw{a + 1}_{T - CHUNK}", align_bytes=BURST)
+            nc.vector.tensor_copy(held[:], token_codes[a][:].indirect(slot_tokens[:, (SLOTS - HELD) // LIST_COL:]))
+            codes[a, E - 1] = held[:]
 
         for a in range(SHARED):
             quantise(a, shared_planes[LIVE * a:P, :])
+            if a >= SPLIT:
+                gather_held(a - 1)
             if a < SHARED - 1:
-                gather_codes(a)
+                gather_codes(a, SLOTS - HELD if a + 1 >= SPLIT else SLOTS)
 
         nc.vector.tensor_copy(slot_planes[:], shared_planes[:].indirect(slot_tokens[:]))
         late_weights = keep.tile([P, (PASSES - EARLY) * PASS_BYTES], U8, name="late_weights", tag="planes_then_weights", align_bytes=BURST)
@@ -166,15 +173,15 @@ def tile_moe_ecr_lin_relu2_kernel(tc, xT, w_words, w_scales, b, gate, offs, pos1
             if a >= EARLY:
                 load_weights(weights[a], a, 0, E)
             move_plane(a)
+        nc.sync.dma_start(token_slots[0][:], pos1)
         load_weights(weights[LAST], LAST, 0, E // 2)
         load_weights(weights[LAST], LAST, E // 2, E)
-        nc.vector.tensor_copy(slot_codes[SHARED - 1][:, 0:SLOTS - HELD],
-                              token_codes[SHARED - 1][:].indirect(slot_tokens[:, 0:(SLOTS - HELD) // LIST_COL]))
+        nc.sync.dma_start(token_slots[1][:], pos2)
+        nc.sync.dma_start(token_slots[2][:], pos3)
+        gather_codes(SHARED - 1, SLOTS - HELD)
 
         sums = [psum.tile([P, C], F32, name=f"sums{e}", tag=f"bank{e}") for e in range(E)]
         pass_planes = [slot_planes] + moved_planes
-
-        codes = {}
 
         def multiply(a, e, scales):
             g = e * PASSES + a
@@ -202,21 +209,17 @@ def tile_moe_ecr_lin_relu2_kernel(tc, xT, w_words, w_scales, b, gate, offs, pos1
 
         quantise(LAST, last_plane[:])
 
-        held_codes = keep.tile([P, HELD], U32, name="held_codes", tag=f"raw{LAST}_{T - CHUNK}", align_bytes=BURST)
-        nc.vector.tensor_copy(held_codes[:], token_codes[SHARED - 1][:].indirect(slot_tokens[:, (SLOTS - HELD) // LIST_COL:]))
-        for e in range(E - HELD // C, E):
-            codes[SHARED - 1, e] = held_codes[:, e * C - (SLOTS - HELD):(e + 1) * C - (SLOTS - HELD)]
-            multiply(SHARED - 1, e, pass_planes[SHARED - 1][:, e * C:(e + 1) * C])
+        gather_held(SHARED - 1)
+        multiply(SHARED - 1, E - 1, pass_planes[SHARED - 1][:, SLOTS - HELD:SLOTS])
 
         gates = keep.tile([P, CHOICES, UPRIGHT], F32, name="gates", tag=f"codes{SHARED - 1}", align_bytes=BURST)
         gate_columns = keep.tile([P, TURNED_BLOCKS, COLUMN_PITCH], F32, name="gate_columns")
+        with nc.allow_non_contiguous_dma(reason="one gate a partition"):
+            for j in range(TURNED_BLOCKS):
+                nc.sync.dma_start(out=gate_columns[:, j, 0:CHOICES],
+                                  in_=gate[:, 0, UPRIGHT + j * P:UPRIGHT + (j + 1) * P].rearrange("r p -> p r"))
         for r in range(CHOICES):
             nc.sync.dma_start(out=gates[:, r, :], in_=gate[r, :, 0:UPRIGHT])
-            if r == 0:
-                with nc.allow_non_contiguous_dma(reason="one gate a partition"):
-                    for j in range(TURNED_BLOCKS):
-                        nc.sync.dma_start(out=gate_columns[:, j, 0:CHOICES],
-                                          in_=gate[:, 0, UPRIGHT + j * P:UPRIGHT + (j + 1) * P].rearrange("r p -> p r"))
 
         gather_codes(LAST)
         clipped = keep.tile([P, SLOTS], F32, name="clipped")

from contextlib import ExitStack

import concourse.mybir as mybir
from concourse.masks import make_identity

K, T, E, C, N = 2560, 768, 6, 128, 128
SLOTS = E * C
PAD = 64
CHOICES = 3
FLOPS = 2 * K * N * SLOTS

F32 = mybir.dt.float32
BF16 = mybir.dt.bfloat16
I32 = mybir.dt.int32
U32 = mybir.dt.uint32
U16 = mybir.dt.uint16
U8 = mybir.dt.uint8
FP8X4 = mybir.dt.float8_e4m3fn_x4
FP4X4 = mybir.dt.float4_e2m1fn_x4
ACT = mybir.ActivationFunctionType
ALU = mybir.AluOpType

P = 128
PACK = 4
K_PASS = P * PACK
PASSES = K // K_PASS
LAST = PASSES - 1
QUADRANT = 32
LIVE = 4
SHARED = 4
STAGED_STEP = QUADRANT // LIVE
LIST_COL = 16
WINDOW = 1024
MOVED_ROWS = 112
BURST = 256
RUN = 2
HELD = C
WARM_UPS = 3
CHUNK = 256
EXPERT_BYTES = 2 * N
PASS_BYTES = E * EXPERT_BYTES
SPLIT = SHARED - 1
EARLY = 2
UPRIGHT_BLOCKS = [256, 256]
UPRIGHT = sum(UPRIGHT_BLOCKS)
TURNED = T - UPRIGHT
TURNED_BLOCKS = TURNED // P
COLUMN_PITCH = 8

VECTOR_TOKENS = 400
LAST_PIECES = [256, 256, 128, 128]


def pieces(widths):
    ranges, start = [], 0
    for width in widths:
        ranges.append((start, start + width))
        start = start + width
    return ranges


def tile_moe_ecr_lin_relu2_kernel(tc, xT, w_words, w_scales, b, gate, offs, pos1, pos2, pos3, out):
    nc = tc.nc

    with ExitStack() as ctx:
        lists = ctx.enter_context(tc.tile_pool(name="lists", bufs=1))
        keep = ctx.enter_context(tc.tile_pool(name="keep", bufs=1))
        psum = ctx.enter_context(tc.psum_pool(name="psum", bufs=1))

        slot_tokens = lists.tile([P, SLOTS // LIST_COL], U16, name="slot_tokens", align_bytes=BURST)
        token_slots = [lists.tile([P, T // LIST_COL], U16, name=f"token_slots{r}", align_bytes=BURST) for r in range(CHOICES)]

        shared_planes = keep.tile([P, WINDOW], U8, name="shared_planes", tag="planes_then_weights", align_bytes=BURST)
        last_plane = keep.tile([P, T], U8, name="last_plane", align_bytes=64)
        token_codes = [keep.tile([P, WINDOW], U32, name=f"token_codes{a}", tag=f"codes{a}", align_bytes=BURST) for a in range(PASSES)]
        moved_planes = [keep.tile([P, SLOTS], U8, name=f"moved_plane{a}", align_bytes=BURST) for a in range(1, SHARED)]
        weight_scales = keep.tile([P, E * PASSES * N], U8, name="weight_scales", align_bytes=BURST)
        y = keep.tile([P, SLOTS + PAD], F32, name="y")
        nc.vector.memset(weight_scales[:].bitcast(I32), 0)
        nc.vector.memset(shared_planes[:].bitcast(I32), 0)
        for a in range(PASSES):
            nc.vector.memset(token_codes[a][:, T:], 0)
        nc.vector.memset(last_plane[:].bitcast(I32), 0)
        for plane in moved_planes:
            nc.vector.memset(plane[:].bitcast(I32), 0)
        nc.vector.memset(y[:, SLOTS:], 0.0)
        identity = keep.tile([P, P], F32, name="identity")
        make_identity(nc, identity[:])

        landings = [pieces([T] if a < SPLIT else [T - CHUNK, CHUNK]) for a in range(PASSES)]
        raw = [[keep.tile([P, PACK, t1 - t0], F32, name=f"raw{a}_{t0}", tag=f"raw{a}_{t0}", align_bytes=BURST) for t0, t1 in landings[a]]
               for a in range(PASSES)]
        for a in range(PASSES):
            if a == LAST:
                nc.sync.dma_start(out=weight_scales[0:P:STAGED_STEP, :].bitcast(I32).rearrange("q (g n) -> q g n", g=E * PASSES),
                                  in_=w_scales.bitcast(I32).rearrange("e a q n -> q (e a) n"))
            for tile, (t0, t1) in zip(raw[a], landings[a]):
                nc.sync.dma_start(out=tile[:], in_=xT[a * K_PASS:(a + 1) * K_PASS, t0:t1].rearrange("(p j) t -> p j t", j=PACK))
            if a == 0:
                nc.sync.dma_start(slot_tokens[:], offs)
        for row in range(1, LIVE):
            nc.sync.dma_start(out=weight_scales[row:P:QUADRANT, :].bitcast(I32),
                              in_=weight_scales[STAGED_STEP * row:P:QUADRANT, :].bitcast(I32))

        def load_weights(dst, a, e0, e1):
            nc.sync.dma_start(out=dst[:, e0 * EXPERT_BYTES:e1 * EXPERT_BYTES].bitcast(I32).rearrange("p (e c) -> p e c", e=e1 - e0),
                              in_=w_words.bitcast(I32).rearrange("e a p c -> a p e c")[a, :, e0:e1, :])

        weights = [keep.tile([P, PASS_BYTES], U8, name=f"weights{a}", align_bytes=BURST)[:] for a in range(EARLY)]
        for a in range(EARLY):
            load_weights(weights[a], a, 0, E)

        bias = keep.tile([P, E], F32, name="bias")
        nc.sync.dma_start(out=bias[:], in_=b)

        def quantise(a, plane):
            chunks = pieces([CHUNK] * (T // CHUNK))
            tags = [f"last_chunk{a - 1}" if a >= SPLIT else f"first_chunk{a}", f"second_chunk{a}", f"last_chunk{a}"]
            grouped = [keep.tile([P, CHUNK, PACK], BF16, name=f"grouped{a}_{i}", tag=tag, align_bytes=64) for i, tag in enumerate(tags)]

            def walk(c0, c1):
                i = c0 // CHUNK
                piece = max(n for n, (t0, t1) in enumerate(landings[a]) if t0 <= c0)
                first = landings[a][piece][0]
                return dict(out=grouped[i][:, c0 - i * CHUNK:c1 - i * CHUNK, :].rearrange("p (c i) j -> p c j i", i=RUN),
                            in_=raw[a][piece][:, :, c0 - first:c1 - first].rearrange("p j (c i) -> p c j i", i=RUN))

            last = T - CHUNK
            if a == 0:
                nc.scalar.activation(func=ACT.Copy, **walk(0, last - VECTOR_TOKENS))
                nc.vector.tensor_copy(**walk(last - VECTOR_TOKENS, CHUNK))
                nc.vector.tensor_copy(**walk(CHUNK, last))
            else:
                nc.gpsimd.tensor_copy(**walk(*chunks[0]))
                nc.scalar.activation(func=ACT.Copy, **walk(*chunks[1]))
            ending = [CHUNK] if a == LAST else [CHUNK // 2, CHUNK // 2]
            for c0, c1 in pieces([last] + ending)[1:]:
                nc.scalar.activation(func=ACT.Copy, **walk(c0, c1))
            for t0, t1 in pieces([CHUNK, CHUNK] + ending):
                i = t0 // CHUNK
                nc.vector.quantize_mx(out=token_codes[a][:, t0:t1].bitcast(FP8X4), scales=plane[:, t0:t1],
                                      in_=grouped[i][:, t0 - i * CHUNK:t1 - i * CHUNK, :].rearrange("p t j -> p (t j)"))

        slot_codes = [keep.tile([P, SLOTS], U32, name=f"slot_codes{a}", align_bytes=64) for a in range(PASSES)]
        slot_planes = keep.tile([P, SLOTS], U8, name="slot_planes", align_bytes=BURST)

        codes = {}

        def gather_codes(a, slots=SLOTS):
            nc.vector.tensor_copy(slot_codes[a][:, 0:slots], token_codes[a][:].indirect(slot_tokens[:, 0:slots // LIST_COL]))

        def gather_held(a):
            held = keep.tile([P, HELD], U32, name=f"held_codes{a}", tag=f"raw{a + 1}_{T - CHUNK}", align_bytes=BURST)
            nc.vector.tensor_copy(held[:], token_codes[a][:].indirect(slot_tokens[:, (SLOTS - HELD) // LIST_COL:]))
            codes[a, E - 1] = held[:]

        for a in range(SHARED):
            quantise(a, shared_planes[LIVE * a:P, :])
            if a >= SPLIT:
                gather_held(a - 1)
            if a < SHARED - 1:
                gather_codes(a, SLOTS - HELD if a + 1 >= SPLIT else SLOTS)

        nc.vector.tensor_copy(slot_planes[:], shared_planes[:].indirect(slot_tokens[:]))
        late_weights = keep.tile([P, (PASSES - EARLY) * PASS_BYTES], U8, name="late_weights", tag="planes_then_weights", align_bytes=BURST)

        def move_plane(a):
            nc.sync.dma_start(out=moved_planes[a - 1][0:MOVED_ROWS, :].bitcast(I32),
                              in_=slot_planes[LIVE * a:LIVE * a + MOVED_ROWS, :].bitcast(I32))

        weights.extend(late_weights[:, i * PASS_BYTES:(i + 1) * PASS_BYTES] for i in range(PASSES - EARLY))
        for a in range(1, SHARED):
            if a >= EARLY:
                load_weights(weights[a], a, 0, E)
            move_plane(a)
        nc.sync.dma_start(token_slots[0][:], pos1)
        load_weights(weights[LAST], LAST, 0, E // 2)
        load_weights(weights[LAST], LAST, E // 2, E)
        nc.sync.dma_start(token_slots[1][:], pos2)
        nc.sync.dma_start(token_slots[2][:], pos3)
        gather_codes(SHARED - 1, SLOTS - HELD)

        sums = [psum.tile([P, C], F32, name=f"sums{e}", tag=f"bank{e}") for e in range(E)]
        pass_planes = [slot_planes] + moved_planes

        def multiply(a, e, scales):
            g = e * PASSES + a
            nc.tensor.matmul_mx(
                out=sums[e][:],
                lhsT=weights[a][:, e * EXPERT_BYTES:(e + 1) * EXPERT_BYTES].bitcast(FP4X4),
                lhsT_scale=weight_scales[:, g * N:(g + 1) * N],
                rhs=codes.get((a, e), slot_codes[a][:, e * C:(e + 1) * C]).bitcast(FP8X4),
                rhs_scale=scales,
                start=(a == 0), stop=(a == LAST))

        for a in range(SHARED):
            for e in range(E if a < SHARED - 1 else E - HELD // C):
                multiply(a, e, pass_planes[a][:, e * C:(e + 1) * C])
            if a == 0:
                idle = psum.tile([P, WARM_UPS, C], F32, name="idle", tag=f"bank{E}")
                for e in range(WARM_UPS):
                    nc.tensor.matmul_mx(
                        out=idle[:, e, :],
                        lhsT=weights[0][:, e * EXPERT_BYTES:(e + 1) * EXPERT_BYTES].bitcast(FP4X4),
                        lhsT_scale=weight_scales[:, e * PASSES * N:(e * PASSES + 1) * N],
                        rhs=slot_codes[0][:, e * C:(e + 1) * C].bitcast(FP8X4),
                        rhs_scale=slot_planes[:, e * C:(e + 1) * C],
                        start=True, stop=True)

        quantise(LAST, last_plane[:])

        gather_held(SHARED - 1)
        multiply(SHARED - 1, E - 1, pass_planes[SHARED - 1][:, SLOTS - HELD:SLOTS])

        gates = keep.tile([P, CHOICES, UPRIGHT], F32, name="gates", tag=f"codes{SHARED - 1}", align_bytes=BURST)
        gate_columns = keep.tile([P, TURNED_BLOCKS, COLUMN_PITCH], F32, name="gate_columns")
        with nc.allow_non_contiguous_dma(reason="one gate a partition"):
            for j in range(TURNED_BLOCKS):
                nc.sync.dma_start(out=gate_columns[:, j, 0:CHOICES],
                                  in_=gate[:, 0, UPRIGHT + j * P:UPRIGHT + (j + 1) * P].rearrange("r p -> p r"))
        for r in range(CHOICES):
            nc.sync.dma_start(out=gates[:, r, :], in_=gate[r, :, 0:UPRIGHT])

        gather_codes(LAST)
        clipped = keep.tile([P, SLOTS], F32, name="clipped")
        for s0, s1 in pieces(LAST_PIECES):
            last_scales = keep.tile([P, s1 - s0], U8, name=f"slot_scales{s0}", align_bytes=64)
            nc.vector.tensor_copy(last_scales[:], last_plane[:].indirect(slot_tokens[:, s0 // LIST_COL:s1 // LIST_COL]))
            for e in range(s0 // C, s1 // C):
                multiply(LAST, e, last_scales[:, e * C - s0:(e + 1) * C - s0])
                nc.scalar.activation(out=clipped[:, e * C:(e + 1) * C], in_=sums[e][:], func=ACT.Relu, bias=bias[:, e:e + 1])
        for s0, s1 in pieces(LAST_PIECES):
            nc.vector.tensor_tensor(y[:, s0:s1], clipped[:, s0:s1], clipped[:, s0:s1], ALU.mult)

        def results(r, t0, t1):
            return y[:].indirect(token_slots[r][:, t0 // LIST_COL:t1 // LIST_COL])

        blocks = pieces([P] * TURNED_BLOCKS)
        summed = [psum.tile([P, P], F32, name=f"summed{j}", tag=f"bank{CHOICES + j}") for j in range(TURNED_BLOCKS)]
        gated = keep.tile([P, CHOICES, TURNED], F32, name="gated")
        turned = [psum.tile([P, TURNED], F32, name=f"turned{r}", tag=f"bank{r}") for r in range(CHOICES)]
        for r in range(CHOICES):
            fetched = keep.tile([P, TURNED], F32, name=f"fetched{r}")
            nc.scalar.activation(out=fetched[:], in_=results(r, UPRIGHT, T), func=ACT.Copy)
            for t0, t1 in blocks:
                nc.tensor.transpose(turned[r][:, t0:t1], fetched[:, t0:t1], identity[:])
            for j, (t0, t1) in enumerate(blocks):
                nc.scalar.activation(out=gated[:, r, t0:t1], in_=turned[r][:, t0:t1], func=ACT.Copy,
                                     scale=gate_columns[:, j, r:r + 1])
                nc.tensor.matmul(summed[j][:], gated[:, r, t0:t1], identity[:], is_transpose=True,
                                 start=(r == 0), stop=(r == CHOICES - 1))
        turned_total = keep.tile([P, TURNED], F32, name="turned_total")
        for j, (t0, t1) in enumerate(blocks):
            nc.scalar.copy(turned_total[:, t0:t1], summed[j][:])
            nc.scalar.dma_start(out=out[:, UPRIGHT + t0:UPRIGHT + t1], in_=turned_total[:, t0:t1])

        terms = [keep.tile([P, UPRIGHT], F32, name=f"term{r}") for r in range(CHOICES)]
        two_terms = keep.tile([P, UPRIGHT], F32, name="two_terms")
        total = keep.tile([P, UPRIGHT], F32, name="total")

        def gated_term(r, t0, t1):
            nc.vector.tensor_tensor(terms[r][:, t0:t1], results(r, t0, t1), gates[:, r, t0:t1], ALU.mult)

        first, second = pieces(UPRIGHT_BLOCKS)
        gated_term(0, 0, UPRIGHT)
        gated_term(1, 0, UPRIGHT)
        gated_term(2, *first)
        nc.vector.tensor_tensor(two_terms[:], terms[0][:], terms[1][:], ALU.add)
        gated_term(2, *second)
        for t0, t1 in (first, second):
            nc.vector.tensor_tensor(total[:, t0:t1], two_terms[:, t0:t1], terms[2][:, t0:t1], ALU.add)
            nc.sync.dma_start(out=out[:, t0:t1], in_=total[:, t0:t1])
